import numpy as np
import ml_dtypes


def mxq(x, axis, fmt="e4m3"):
    dtype, down = {"e4m3": (ml_dtypes.float8_e4m3fn, 7), "e5m2": (ml_dtypes.float8_e5m2, 14)}[fmt]
    v = np.moveaxis(np.asarray(x, np.float32).astype(ml_dtypes.bfloat16).astype(np.float64), axis, -1)
    blocks = v.reshape(v.shape[:-1] + (-1, 32))
    amax = np.abs(blocks).max(-1, keepdims=True)
    byte = np.maximum(np.where(amax > 0, np.frexp(amax)[1] - 1 + 127, 0) - down, 1)
    scale = np.exp2(byte - 127.0)
    codes = (blocks / scale).astype(np.float32).astype(dtype).astype(np.float64)
    return np.moveaxis((codes * scale).reshape(v.shape), -1, axis)


WIDE = False


def mx_kscale(k):
    if not WIDE:
        return np.ones(k)
    levels = np.array([10, -10, 5, -5, 0])
    if k % 512:
        return np.exp2(np.random.permutation(np.resize(levels, k // 32))).repeat(32)
    a = np.empty((k // 512, 16))
    for p in range(k // 512):
        a[p, :8] = np.random.permutation(np.resize(levels, 8))
        for g in range(8):
            far = levels[np.abs(levels - a[p, g]) >= 10]
            a[p, g + 8] = far[np.random.randint(len(far))]
    return np.exp2(a.ravel()).repeat(32)


def f64(x):
    return np.asarray(x).astype(np.float64)


def striped(idx):
    return np.tile(idx.reshape(-1, 16).T, (8, 1)).astype(np.uint16)


def unstriped(offs):
    return offs[:16].T.reshape(-1).astype(np.int64)


def pack_weight(w):
    k, n = w.shape
    w = f64(np.asarray(w, np.float32).astype(ml_dtypes.bfloat16)).reshape(k // 32, 32, n)
    amax = np.abs(w).max(1)
    byte = np.clip(np.where(amax > 0, np.frexp(amax)[1] - 1 + 127 - 7, 1), 1, 254)
    scaled = (w * np.exp2(127.0 - byte)[:, None, :]).reshape(k, n).astype(np.float32)
    words = np.ascontiguousarray(scaled.reshape(k // 512, 128, 4, n).transpose(0, 1, 3, 2)).astype(ml_dtypes.float8_e4m3fn).view(np.uint8)
    return words, np.ascontiguousarray(byte.astype(np.uint8).reshape(k // 512, 16, n))


def unpack_weight(words, scales):
    g, p, n, _ = words.shape
    vals = np.ascontiguousarray(words).view(ml_dtypes.float8_e4m3fn).astype(np.float64) * np.repeat(np.exp2(scales.astype(np.float64) - 127.0), 8, axis=1)[..., None]
    return vals.transpose(0, 1, 3, 2).reshape(g * 512, n)


def gelu(v):
    return 0.5 * v * (1.0 + np.tanh(np.sqrt(2.0 / np.pi) * (v + 0.044715 * v**3)))


K, T, D, S, V, N = 1536, 2048, 8, 512, 64, 256


def setup_inputs():
    n = np.random.standard_normal
    s = mx_kscale(K)[:, None]
    words, scales = pack_weight(n((K, N)) / np.sqrt(K) / s)
    return {
        "xT": (n((K, T)) * s).astype(np.float32),
        "w_words": words,
        "w_scales": scales,
        "b": (0.3 * n((N, 1))).astype(np.float32),
        "offs": striped(np.random.permutation(T)[:S]),
    }


def reference(xT, w_words, w_scales, b, offs):
    w = unpack_weight(w_words, w_scales)
    idx = unstriped(offs)
    xq = mxq(f64(xT)[:, idx], 0, "e4m3")
    y = w.T @ xq
    y = gelu(y + f64(b))
    return y.reshape(N, V, D).max(axis=2)

@@ -1,0 +1,155 @@
+from contextlib import ExitStack
+
+import concourse.mybir as mybir
+
+K, T, S, N, D = 1536, 2048, 512, 256, 8
+FLOPS = 2 * K * S * N
+
+F32 = mybir.dt.float32
+BF16 = mybir.dt.bfloat16
+U32 = mybir.dt.uint32
+I32 = mybir.dt.int32
+U16 = mybir.dt.uint16
+U8 = mybir.dt.uint8
+FP8X4 = mybir.dt.float8_e4m3fn_x4
+GELU = mybir.ActivationFunctionType.Gelu_apprx_tanh
+
+P = 128
+PACK = 4
+PASSES = K // (P * PACK)
+M_TILES = N // P
+HALF = S // 2
+COLS = HALF // 16
+LOADS = (((0, 2), (2, 4)), ((0, 2), (2, 3), (3, 4)), ((0, 1), (1, 2), (2, 3), (3, 4)))
+
+
+def tile_picked_pool_lin_gelu_sub_e_kernel(tc, xT, w_words, w_scales, b, offs, out):
+    nc = tc.nc
+    with ExitStack() as ctx:
+        keep = ctx.enter_context(tc.tile_pool(name="keep", bufs=1))
+        psum = ctx.enter_context(tc.psum_pool(name="psum", bufs=1))
+
+        offsets = keep.tile([P, S // 16], U16, name="offsets")
+        w_codes = keep.tile([P, PASSES, N], I32, name="w_codes", align_bytes=64)
+        w_scale = keep.tile([P, PASSES, N], U8, name="w_scale", align_bytes=64)
+        bias = keep.tile([P, M_TILES], F32, name="bias")
+        warm = keep.tile([P, 1], F32, name="warm")
+        pooled = keep.tile([P, M_TILES, S // D], F32, name="pooled")
+
+        blocks = [
+            [keep.tile([P, last - first, T], F32, name=f"x_{a}_{first}") for first, last in LOADS[a]]
+            for a in range(PASSES)
+        ]
+        grouped = [keep.tile([P, S, PACK], BF16, name=f"grouped_{a}", align_bytes=64) for a in range(PASSES)]
+        codes = [keep.tile([P, S], U32, name=f"codes_{a}", align_bytes=64) for a in range(PASSES)]
+        scales = [keep.tile([P, S], U8, name=f"scales_{a}", align_bytes=64) for a in range(PASSES)]
+        acc = [[psum.tile([P, HALF], F32, name=f"acc_{m}_{s}") for s in range(2)] for m in range(M_TILES)]
+        scratch = psum.tile([P, HALF], F32, name="scratch")
+        act = [[keep.tile([P, HALF], F32, name=f"act_{m}_{s}") for s in range(2)] for m in range(M_TILES)]
+
+        nc.vector.memset(w_scale[:].bitcast(I32), 0)
+        nc.vector.memset(warm[:], 0.0)
+        nc.scalar.activation(warm[:], warm[:], GELU)
+
+        x_view = xT.rearrange("(a p j) t -> a p j t", p=P, j=PACK)
+        w_view = w_words.rearrange("a p m r -> p a (m r)").bitcast(I32)
+
+        def load_block(a, i):
+            first, last = LOADS[a][i]
+            nc.sync.dma_start(out=blocks[a][i][:], in_=x_view[a, :, first:last, :])
+
+        def plane(a, j):
+            for (first, last), block in zip(LOADS[a], blocks[a]):
+                if first <= j < last:
+                    return block[:, j - first, :]
+
+        def load_weights(first, last):
+            nc.sync.dma_start(out=w_codes[:, first:last, :], in_=w_view[:, first:last, :])
+
+        def load_scales(first, last):
+            for q in range(4):
+                nc.sync.dma_start(
+                    out=w_scale[32 * q : 32 * q + 4, first:last, :].bitcast(I32),
+                    in_=w_scales[first:last, 4 * q : 4 * q + 4, :].rearrange("a r m -> r a m").bitcast(I32),
+                )
+
+        nc.sync.dma_start(offsets[:], offs)
+        for a, i in ((0, 0), (0, 1), (1, 0), (1, 1), (2, 0), (2, 1), (2, 2), (1, 2), (2, 3)):
+            load_block(a, i)
+        load_scales(0, PASSES)
+        load_weights(0, 1)
+        load_weights(1, PASSES)
+        with nc.allow_non_contiguous_dma(reason="one bias value a partition"):
+            nc.sync.dma_start(out=bias[:], in_=b.rearrange("(m p) o -> p (m o)", p=P))
+
+        def multiply(a, s):
+            cols = slice(s * HALF, (s + 1) * HALF)
+            for m in range(M_TILES):
+                rows = slice(m * P, (m + 1) * P)
+                nc.tensor.matmul_mx(
+                    out=acc[m][s][:],
+                    lhsT=w_codes[:, a, rows].bitcast(FP8X4),
+                    lhsT_scale=w_scale[:, a, rows],
+                    rhs=codes[a][:, cols].bitcast(FP8X4),
+                    rhs_scale=scales[a][:, cols],
+                    start=(a == 0),
+                    stop=(a == PASSES - 1),
+                )
+
+        def quantize(a, first, last):
+            nc.vector.quantize_mx(
+                out=codes[a][:, first:last].bitcast(FP8X4),
+                scales=scales[a][:, first:last],
+                in_=grouped[a][:, first:last, :].rearrange("p n j -> p (n j)"),
+            )
+
+        def gather(a, j):
+            nc.vector.tensor_copy(grouped[a][:, :, j], plane(a, j).indirect(offsets[:]))
+
+        def gather_half(a, s):
+            nc.vector.tensor_copy(
+                grouped[a][:, s * HALF : (s + 1) * HALF, PACK - 1],
+                plane(a, PACK - 1).indirect(offsets[:, s * COLS : (s + 1) * COLS]),
+            )
+
+        for j in range(PACK):
+            gather(0, j)
+        quantize(0, 0, S)
+        for j in range(PACK - 1):
+            gather(1, j)
+        for j in range(PACK - 1):
+            gather(2, j)
+        gather_half(1, 0)
+        gather_half(1, 1)
+        quantize(1, 0, HALF)
+        for i in range(3):
+            nc.tensor.matmul_mx(
+                out=scratch[:],
+                lhsT=codes[1][:, 0:P].bitcast(FP8X4),
+                lhsT_scale=scales[1][:, 0:P],
+                rhs=codes[1][:, 0:HALF].bitcast(FP8X4),
+                rhs_scale=scales[1][:, 0:HALF],
+                start=True,
+                stop=True,
+            )
+        quantize(1, HALF, S)
+        for a in range(PASSES - 1):
+            for s in range(2):
+                multiply(a, s)
+        a = PASSES - 1
+        for s in range(2):
+            gather_half(a, s)
+        for s in range(2):
+            quantize(a, s * HALF, (s + 1) * HALF)
+            multiply(a, s)
+        out_view = out.rearrange("(m p) v -> p m v", p=P)
+        for s in range(2):
+            for m in range(M_TILES):
+                nc.scalar.activation(act[m][s][:], acc[m][s][:], GELU, bias=bias[:, m : m + 1])
+                nc.vector.tensor_reduce(
+                    out=pooled[:, m, s * HALF // D : (s + 1) * HALF // D],
+                    in_=act[m][s][:].rearrange("p (v d) -> p v d", d=D),
+                    op=mybir.AluOpType.max,
+                    axis=mybir.AxisListType.X,
+                )
+        nc.sync.dma_start(out=out_view, in_=pooled[:])

@@ -20,6 +20,8 @@ PASSES = K // (P * PACK)
 M_TILES = N // P
 HALF = S // 2
 COLS = HALF // 16
+PART = 128
+PARTS = S // PART
 LOADS = (((0, 2), (2, 4)), ((0, 2), (2, 3), (3, 4)), ((0, 1), (1, 2), (2, 3), (3, 4)))
 
 
@@ -30,7 +32,7 @@ def tile_picked_pool_lin_gelu_sub_e_kernel(tc, xT, w_words, w_scales, b, offs, o
         psum = ctx.enter_context(tc.psum_pool(name="psum", bufs=1))
 
         offsets = keep.tile([P, S // 16], U16, name="offsets")
-        w_codes = keep.tile([P, PASSES, N], I32, name="w_codes", align_bytes=64)
+        w_codes = [keep.tile([P, N], I32, name=f"w_codes_{a}", align_bytes=64) for a in range(PASSES)]
         w_scale = keep.tile([P, PASSES, N], U8, name="w_scale", align_bytes=64)
         bias = keep.tile([P, M_TILES], F32, name="bias")
         warm = keep.tile([P, 1], F32, name="warm")
@@ -43,16 +45,15 @@ def tile_picked_pool_lin_gelu_sub_e_kernel(tc, xT, w_words, w_scales, b, offs, o
         grouped = [keep.tile([P, S, PACK], BF16, name=f"grouped_{a}", align_bytes=64) for a in range(PASSES)]
         codes = [keep.tile([P, S], U32, name=f"codes_{a}", align_bytes=64) for a in range(PASSES)]
         scales = [keep.tile([P, S], U8, name=f"scales_{a}", align_bytes=64) for a in range(PASSES)]
-        acc = [[psum.tile([P, HALF], F32, name=f"acc_{m}_{s}") for s in range(2)] for m in range(M_TILES)]
-        scratch = psum.tile([P, HALF], F32, name="scratch")
-        act = [[keep.tile([P, HALF], F32, name=f"act_{m}_{s}") for s in range(2)] for m in range(M_TILES)]
+        acc = [[psum.tile([P, PART], F32, name=f"acc_{m}_{s}") for s in range(PARTS)] for m in range(M_TILES)]
+        act = [[keep.tile([P, PART], F32, name=f"act_{m}_{s}") for s in range(PARTS)] for m in range(M_TILES)]
 
         nc.vector.memset(w_scale[:].bitcast(I32), 0)
         nc.vector.memset(warm[:], 0.0)
         nc.scalar.activation(warm[:], warm[:], GELU)
 
         x_view = xT.rearrange("(a p j) t -> a p j t", p=P, j=PACK)
-        w_view = w_words.rearrange("a p m r -> p a (m r)").bitcast(I32)
+        w_view = w_words.rearrange("a p m r -> a p (m r)").bitcast(I32)
 
         def load_block(a, i):
             first, last = LOADS[a][i]
@@ -63,32 +64,35 @@ def tile_picked_pool_lin_gelu_sub_e_kernel(tc, xT, w_words, w_scales, b, offs, o
                 if first <= j < last:
                     return block[:, j - first, :]
 
-        def load_weights(first, last):
-            nc.sync.dma_start(out=w_codes[:, first:last, :], in_=w_view[:, first:last, :])
+        def load_weights(a):
+            nc.sync.dma_start(out=w_codes[a][:], in_=w_view[a])
 
-        def load_scales(first, last):
+        def load_scales():
             for q in range(4):
                 nc.sync.dma_start(
-                    out=w_scale[32 * q : 32 * q + 4, first:last, :].bitcast(I32),
-                    in_=w_scales[first:last, 4 * q : 4 * q + 4, :].rearrange("a r m -> r a m").bitcast(I32),
+                    out=w_scale[32 * q : 32 * q + 4, :, :].bitcast(I32),
+                    in_=w_scales[:, 4 * q : 4 * q + 4, :].rearrange("a r m -> r a m").bitcast(I32),
                 )
 
+        load_block(0, 0)
         nc.sync.dma_start(offsets[:], offs)
-        for a, i in ((0, 0), (0, 1), (1, 0), (1, 1), (2, 0), (2, 1), (2, 2), (1, 2), (2, 3)):
+        load_scales()
+        for a, i in ((0, 1), (1, 0), (1, 1), (1, 2), (2, 0), (2, 1), (2, 2)):
             load_block(a, i)
-        load_scales(0, PASSES)
-        load_weights(0, 1)
-        load_weights(1, PASSES)
+        load_weights(0)
+        load_block(2, 3)
+        load_weights(1)
+        load_weights(2)
         with nc.allow_non_contiguous_dma(reason="one bias value a partition"):
             nc.sync.dma_start(out=bias[:], in_=b.rearrange("(m p) o -> p (m o)", p=P))
 
         def multiply(a, s):
-            cols = slice(s * HALF, (s + 1) * HALF)
+            cols = slice(s * PART, (s + 1) * PART)
             for m in range(M_TILES):
                 rows = slice(m * P, (m + 1) * P)
                 nc.tensor.matmul_mx(
                     out=acc[m][s][:],
-                    lhsT=w_codes[:, a, rows].bitcast(FP8X4),
+                    lhsT=w_codes[a][:, rows].bitcast(FP8X4),
                     lhsT_scale=w_scale[:, a, rows],
                     rhs=codes[a][:, cols].bitcast(FP8X4),
                     rhs_scale=scales[a][:, cols],
@@ -112,42 +116,28 @@ def tile_picked_pool_lin_gelu_sub_e_kernel(tc, xT, w_words, w_scales, b, offs, o
                 plane(a, PACK - 1).indirect(offsets[:, s * COLS : (s + 1) * COLS]),
             )
 
-        for j in range(PACK):
-            gather(0, j)
-        quantize(0, 0, S)
-        for j in range(PACK - 1):
-            gather(1, j)
-        for j in range(PACK - 1):
-            gather(2, j)
-        gather_half(1, 0)
-        gather_half(1, 1)
-        quantize(1, 0, HALF)
-        for i in range(3):
-            nc.tensor.matmul_mx(
-                out=scratch[:],
-                lhsT=codes[1][:, 0:P].bitcast(FP8X4),
-                lhsT_scale=scales[1][:, 0:P],
-                rhs=codes[1][:, 0:HALF].bitcast(FP8X4),
-                rhs_scale=scales[1][:, 0:HALF],
-                start=True,
-                stop=True,
-            )
-        quantize(1, HALF, S)
         for a in range(PASSES - 1):
-            for s in range(2):
+            for j in range(PACK):
+                gather(a, j)
+            quantize(a, 0, S)
+        a = PASSES - 1
+        for j in range(PACK - 1):
+            gather(a, j)
+        for a in range(PASSES - 1):
+            for s in range(PARTS):
                 multiply(a, s)
         a = PASSES - 1
         for s in range(2):
             gather_half(a, s)
-        for s in range(2):
-            quantize(a, s * HALF, (s + 1) * HALF)
+        for s in range(PARTS):
+            quantize(a, s * PART, (s + 1) * PART)
             multiply(a, s)
         out_view = out.rearrange("(m p) v -> p m v", p=P)
-        for s in range(2):
+        for s in range(PARTS):
             for m in range(M_TILES):
                 nc.scalar.activation(act[m][s][:], acc[m][s][:], GELU, bias=bias[:, m : m + 1])
                 nc.vector.tensor_reduce(
-                    out=pooled[:, m, s * HALF // D : (s + 1) * HALF // D],
+                    out=pooled[:, m, s * PART // D : (s + 1) * PART // D],
                     in_=act[m][s][:].rearrange("p (v d) -> p v d", d=D),
                     op=mybir.AluOpType.max,
                     axis=mybir.AxisListType.X,

@@ -22,7 +22,8 @@ HALF = S // 2
 COLS = HALF // 16
 PART = 128
 PARTS = S // PART
-LOADS = (((0, 2), (2, 4)), ((0, 2), (2, 3), (3, 4)), ((0, 1), (1, 2), (2, 3), (3, 4)))
+LOADS = (((0, 4),), ((0, 2), (2, 4)), ((0, 2), (2, 3), (3, 4)))
+PAIR = 2
 
 
 def tile_picked_pool_lin_gelu_sub_e_kernel(tc, xT, w_words, w_scales, b, offs, out):
@@ -43,6 +44,7 @@ def tile_picked_pool_lin_gelu_sub_e_kernel(tc, xT, w_words, w_scales, b, offs, o
             for a in range(PASSES)
         ]
         grouped = [keep.tile([P, S, PACK], BF16, name=f"grouped_{a}", align_bytes=64) for a in range(PASSES)]
+        picked = [keep.tile([P, PAIR, S], F32, name=f"picked_{a}") for a in range(PASSES)]
         codes = [keep.tile([P, S], U32, name=f"codes_{a}", align_bytes=64) for a in range(PASSES)]
         scales = [keep.tile([P, S], U8, name=f"scales_{a}", align_bytes=64) for a in range(PASSES)]
         acc = [[psum.tile([P, PART], F32, name=f"acc_{m}_{s}") for s in range(PARTS)] for m in range(M_TILES)]
@@ -77,10 +79,10 @@ def tile_picked_pool_lin_gelu_sub_e_kernel(tc, xT, w_words, w_scales, b, offs, o
         load_block(0, 0)
         nc.sync.dma_start(offsets[:], offs)
         load_scales()
-        for a, i in ((0, 1), (1, 0), (1, 1), (1, 2), (2, 0), (2, 1), (2, 2)):
+        for a, i in ((1, 0), (1, 1), (2, 0), (2, 1)):
             load_block(a, i)
         load_weights(0)
-        load_block(2, 3)
+        load_block(2, 2)
         load_weights(1)
         load_weights(2)
         with nc.allow_non_contiguous_dma(reason="one bias value a partition"):
@@ -110,6 +112,11 @@ def tile_picked_pool_lin_gelu_sub_e_kernel(tc, xT, w_words, w_scales, b, offs, o
         def gather(a, j):
             nc.vector.tensor_copy(grouped[a][:, :, j], plane(a, j).indirect(offsets[:]))
 
+        def gather_pair(a):
+            for j in range(PAIR):
+                nc.vector.tensor_copy(picked[a][:, j, :], plane(a, j).indirect(offsets[:]))
+            nc.scalar.copy(grouped[a][:, :, 0:PAIR], picked[a][:].rearrange("p j n -> p n j"))
+
         def gather_half(a, s):
             nc.vector.tensor_copy(
                 grouped[a][:, s * HALF : (s + 1) * HALF, PACK - 1],
@@ -117,12 +124,13 @@ def tile_picked_pool_lin_gelu_sub_e_kernel(tc, xT, w_words, w_scales, b, offs, o
             )
 
         for a in range(PASSES - 1):
-            for j in range(PACK):
+            gather_pair(a)
+            for j in range(PAIR, PACK):
                 gather(a, j)
             quantize(a, 0, S)
         a = PASSES - 1
-        for j in range(PACK - 1):
-            gather(a, j)
+        gather_pair(a)
+        gather(a, PAIR)
         for a in range(PASSES - 1):
             for s in range(PARTS):
                 multiply(a, s)

@@ -19,11 +19,12 @@ PACK = 4
 PASSES = K // (P * PACK)
 M_TILES = N // P
 HALF = S // 2
-COLS = HALF // 16
 PART = 128
 PARTS = S // PART
 LOADS = (((0, 4),), ((0, 2), (2, 4)), ((0, 2), (2, 3), (3, 4)))
 PAIR = 2
+ORDER = (0, 2, 3, 1)
+SLICES = ((0, PART), (PART, HALF))
 
 
 def tile_picked_pool_lin_gelu_sub_e_kernel(tc, xT, w_words, w_scales, b, offs, out):
@@ -37,15 +38,18 @@ def tile_picked_pool_lin_gelu_sub_e_kernel(tc, xT, w_words, w_scales, b, offs, o
         w_scale = keep.tile([P, PASSES, N], U8, name="w_scale", align_bytes=64)
         bias = keep.tile([P, M_TILES], F32, name="bias")
         warm = keep.tile([P, 1], F32, name="warm")
-        pooled = keep.tile([P, M_TILES, S // D], F32, name="pooled")
 
         blocks = [
-            [keep.tile([P, last - first, T], F32, name=f"x_{a}_{first}") for first, last in LOADS[a]]
+            [keep.tile([P, (last - first) * T], F32, name=f"x_{a}_{first}") for first, last in LOADS[a]]
             for a in range(PASSES)
         ]
-        grouped = [keep.tile([P, S, PACK], BF16, name=f"grouped_{a}", align_bytes=64) for a in range(PASSES)]
+        grouped = [keep.tile([P, S, PACK], BF16, name=f"grouped_{a}", align_bytes=64) for a in range(PASSES - 1)]
         picked = [keep.tile([P, PAIR, S], F32, name=f"picked_{a}") for a in range(PASSES)]
-        codes = [keep.tile([P, S], U32, name=f"codes_{a}", align_bytes=64) for a in range(PASSES)]
+        late = [keep.tile([P, PAIR * (last - first)], BF16, name=f"late_{first}", tag=f"late_{first}", align_bytes=64) for first, last in SLICES]
+        ends = [keep.tile([P, PART, PACK], BF16, name=f"ends_{s}", tag=f"ends_{s}", align_bytes=64)[:] for s in range(2)]
+        upper = keep.tile([P, HALF, PACK], BF16, name="upper", align_bytes=64)
+        ends = ends + [upper[:, s * PART : (s + 1) * PART, :] for s in range(2)]
+        codes = {}
         scales = [keep.tile([P, S], U8, name=f"scales_{a}", align_bytes=64) for a in range(PASSES)]
         acc = [[psum.tile([P, PART], F32, name=f"acc_{m}_{s}") for s in range(PARTS)] for m in range(M_TILES)]
         act = [[keep.tile([P, PART], F32, name=f"act_{m}_{s}") for s in range(PARTS)] for m in range(M_TILES)]
@@ -54,17 +58,17 @@ def tile_picked_pool_lin_gelu_sub_e_kernel(tc, xT, w_words, w_scales, b, offs, o
         nc.vector.memset(warm[:], 0.0)
         nc.scalar.activation(warm[:], warm[:], GELU)
 
-        x_view = xT.rearrange("(a p j) t -> a p j t", p=P, j=PACK)
+        x_view = xT.rearrange("(a p j) t -> a p (j t)", p=P, j=PACK)
         w_view = w_words.rearrange("a p m r -> a p (m r)").bitcast(I32)
 
         def load_block(a, i):
             first, last = LOADS[a][i]
-            nc.sync.dma_start(out=blocks[a][i][:], in_=x_view[a, :, first:last, :])
+            nc.sync.dma_start(out=blocks[a][i][:], in_=x_view[a, :, first * T : last * T])
 
         def plane(a, j):
             for (first, last), block in zip(LOADS[a], blocks[a]):
                 if first <= j < last:
-                    return block[:, j - first, :]
+                    return block[:, (j - first) * T : (j - first + 1) * T]
 
         def load_weights(a):
             nc.sync.dma_start(out=w_codes[a][:], in_=w_view[a])
@@ -96,17 +100,19 @@ def tile_picked_pool_lin_gelu_sub_e_kernel(tc, xT, w_words, w_scales, b, offs, o
                     out=acc[m][s][:],
                     lhsT=w_codes[a][:, rows].bitcast(FP8X4),
                     lhsT_scale=w_scale[:, a, rows],
-                    rhs=codes[a][:, cols].bitcast(FP8X4),
+                    rhs=codes[a, s].bitcast(FP8X4),
                     rhs_scale=scales[a][:, cols],
                     start=(a == 0),
                     stop=(a == PASSES - 1),
                 )
 
-        def quantize(a, first, last):
+        def quantize(a, first, last, values, words):
+            for s in range(first // PART, last // PART):
+                codes[a, s] = words[:, s * PART - first : (s + 1) * PART - first]
             nc.vector.quantize_mx(
-                out=codes[a][:, first:last].bitcast(FP8X4),
+                out=words.bitcast(FP8X4),
                 scales=scales[a][:, first:last],
-                in_=grouped[a][:, first:last, :].rearrange("p n j -> p (n j)"),
+                in_=values.rearrange("p n j -> p (n j)"),
             )
 
         def gather(a, j):
@@ -115,33 +121,53 @@ def tile_picked_pool_lin_gelu_sub_e_kernel(tc, xT, w_words, w_scales, b, offs, o
         def gather_pair(a):
             for j in range(PAIR):
                 nc.vector.tensor_copy(picked[a][:, j, :], plane(a, j).indirect(offsets[:]))
-            nc.scalar.copy(grouped[a][:, :, 0:PAIR], picked[a][:].rearrange("p j n -> p n j"))
 
-        def gather_half(a, s):
-            nc.vector.tensor_copy(
-                grouped[a][:, s * HALF : (s + 1) * HALF, PACK - 1],
-                plane(a, PACK - 1).indirect(offsets[:, s * COLS : (s + 1) * COLS]),
-            )
+        def gather_late(j):
+            for (first, last), tile in zip(SLICES, late):
+                width = last - first
+                nc.vector.tensor_copy(
+                    tile[:, (j - PAIR) * width : (j - PAIR + 1) * width],
+                    blocks[PASSES - 1][j - 1][:].indirect(offsets[:, first // 16 : last // 16]),
+                )
+            nc.vector.tensor_copy(upper[:, :, j], plane(PASSES - 1, j).indirect(offsets[:, HALF // 16 : S // 16]))
+
+        def weave_late(s, copy):
+            for (first, last), tile in zip(SLICES, late):
+                if first <= s * PART < last:
+                    cols = slice(s * PART - first, (s + 1) * PART - first)
+                    copy(ends[s][:, :, PAIR:PACK], tile[:].rearrange("p (j n) -> p n j", j=PAIR)[:, cols, :])
 
         for a in range(PASSES - 1):
             gather_pair(a)
+            nc.scalar.copy(grouped[a][:, :, 0:PAIR], picked[a][:].rearrange("p j n -> p n j"))
             for j in range(PAIR, PACK):
                 gather(a, j)
-            quantize(a, 0, S)
+            words = keep.tile([P, S], U32, name=f"codes_{a}", align_bytes=64)
+            quantize(a, 0, S, grouped[a][:], words[:])
         a = PASSES - 1
         gather_pair(a)
-        gather(a, PAIR)
+        for s in range(PARTS):
+            nc.scalar.copy(
+                ends[s][:, :, 0:PAIR],
+                picked[a][:, :, s * PART : (s + 1) * PART].rearrange("p j n -> p n j"),
+            )
+        gather_late(2)
         for a in range(PASSES - 1):
             for s in range(PARTS):
                 multiply(a, s)
         a = PASSES - 1
+        gather_late(3)
         for s in range(2):
-            gather_half(a, s)
-        for s in range(PARTS):
-            quantize(a, s * PART, (s + 1) * PART)
+            weave_late(s, nc.scalar.copy)
+        lower_words = keep.tile([P, HALF], U32, name="lower_words", align_bytes=64)
+        upper_words = keep.tile([P, HALF], U32, name="upper_words", tag="late_0", align_bytes=64)
+        for s in ORDER:
+            words = (lower_words, upper_words)[s // 2]
+            quantize(a, s * PART, (s + 1) * PART, ends[s], words[:, s % 2 * PART : (s % 2 + 1) * PART])
             multiply(a, s)
+        pooled = keep.tile([P, M_TILES, S // D], F32, name="pooled", tag="ends_1", align_bytes=64)
         out_view = out.rearrange("(m p) v -> p m v", p=P)
-        for s in range(PARTS):
+        for s in ORDER:
             for m in range(M_TILES):
                 nc.scalar.activation(act[m][s][:], acc[m][s][:], GELU, bias=bias[:, m : m + 1])
                 nc.vector.tensor_reduce(

@@ -25,6 +25,8 @@ LOADS = (((0, 4),), ((0, 2), (2, 4)), ((0, 2), (2, 3), (3, 4)))
 PAIR = 2
 ORDER = (0, 2, 3, 1)
 SLICES = ((0, PART), (PART, HALF))
+WARM_UPS = 3
+WARM_ROWS = 32
 
 
 def tile_picked_pool_lin_gelu_sub_e_kernel(tc, xT, w_words, w_scales, b, offs, out):
@@ -40,7 +42,7 @@ def tile_picked_pool_lin_gelu_sub_e_kernel(tc, xT, w_words, w_scales, b, offs, o
         warm = keep.tile([P, 1], F32, name="warm")
 
         blocks = [
-            [keep.tile([P, (last - first) * T], F32, name=f"x_{a}_{first}") for first, last in LOADS[a]]
+            [keep.tile([P, (last - first) * T], F32, name=f"x_{a}_{first}", tag=f"x_{a}_{first}", align_bytes=64) for first, last in LOADS[a]]
             for a in range(PASSES)
         ]
         grouped = [keep.tile([P, S, PACK], BF16, name=f"grouped_{a}", align_bytes=64) for a in range(PASSES - 1)]
@@ -51,7 +53,8 @@ def tile_picked_pool_lin_gelu_sub_e_kernel(tc, xT, w_words, w_scales, b, offs, o
         ends = ends + [upper[:, s * PART : (s + 1) * PART, :] for s in range(2)]
         codes = {}
         scales = [keep.tile([P, S], U8, name=f"scales_{a}", align_bytes=64) for a in range(PASSES)]
-        acc = [[psum.tile([P, PART], F32, name=f"acc_{m}_{s}") for s in range(PARTS)] for m in range(M_TILES)]
+        banks = [[psum.tile([P, S], F32, name=f"acc_{m}_{s}") for s in range(PARTS)] for m in range(M_TILES)]
+        acc = [[bank[:, 0:PART] for bank in row] for row in banks]
         act = [[keep.tile([P, PART], F32, name=f"act_{m}_{s}") for s in range(PARTS)] for m in range(M_TILES)]
 
         nc.vector.memset(w_scale[:].bitcast(I32), 0)
@@ -83,12 +86,10 @@ def tile_picked_pool_lin_gelu_sub_e_kernel(tc, xT, w_words, w_scales, b, offs, o
         load_block(0, 0)
         nc.sync.dma_start(offsets[:], offs)
         load_scales()
-        for a, i in ((1, 0), (1, 1), (2, 0), (2, 1)):
+        for a, i in ((1, 0), (1, 1), (2, 0), (2, 1), (2, 2)):
             load_block(a, i)
-        load_weights(0)
-        load_block(2, 2)
-        load_weights(1)
-        load_weights(2)
+        for a in range(PASSES):
+            load_weights(a)
         with nc.allow_non_contiguous_dma(reason="one bias value a partition"):
             nc.sync.dma_start(out=bias[:], in_=b.rearrange("(m p) o -> p (m o)", p=P))
 
@@ -97,7 +98,7 @@ def tile_picked_pool_lin_gelu_sub_e_kernel(tc, xT, w_words, w_scales, b, offs, o
             for m in range(M_TILES):
                 rows = slice(m * P, (m + 1) * P)
                 nc.tensor.matmul_mx(
-                    out=acc[m][s][:],
+                    out=acc[m][s],
                     lhsT=w_codes[a][:, rows].bitcast(FP8X4),
                     lhsT_scale=w_scale[:, a, rows],
                     rhs=codes[a, s].bitcast(FP8X4),
@@ -143,7 +144,12 @@ def tile_picked_pool_lin_gelu_sub_e_kernel(tc, xT, w_words, w_scales, b, offs, o
             for j in range(PAIR, PACK):
                 gather(a, j)
             words = keep.tile([P, S], U32, name=f"codes_{a}", align_bytes=64)
-            quantize(a, 0, S, grouped[a][:], words[:])
+            if a == 0:
+                first_words = words
+                quantize(a, 0, S, grouped[a][:], words[:])
+            else:
+                quantize(a, 0, PART, grouped[a][:, 0:PART, :], words[:, 0:PART])
+                quantize(a, HALF, S, grouped[a][:, HALF:S, :], words[:, HALF:S])
         a = PASSES - 1
         gather_pair(a)
         for s in range(PARTS):
@@ -152,16 +158,29 @@ def tile_picked_pool_lin_gelu_sub_e_kernel(tc, xT, w_words, w_scales, b, offs, o
                 picked[a][:, :, s * PART : (s + 1) * PART].rearrange("p j n -> p n j"),
             )
         gather_late(2)
-        for a in range(PASSES - 1):
-            for s in range(PARTS):
-                multiply(a, s)
-        a = PASSES - 1
+        held = keep.tile([P, PART], U32, name="held", tag="x_2_0", align_bytes=64)
+        quantize(1, PART, HALF, grouped[1][:, PART:HALF, :], held[:])
+        for i in range(WARM_UPS):
+            nc.tensor.matmul_mx(
+                out=banks[1][1][0:WARM_ROWS, :],
+                lhsT=held[:, 0:WARM_ROWS].bitcast(FP8X4),
+                lhsT_scale=scales[1][:, PART : PART + WARM_ROWS],
+                rhs=first_words[:].bitcast(FP8X4),
+                rhs_scale=scales[0][:],
+                start=True,
+                stop=True,
+            )
+        for a, s in ((0, 0), (0, 2), (1, 0), (1, 2), (0, 3)):
+            multiply(a, s)
         gather_late(3)
         for s in range(2):
             weave_late(s, nc.scalar.copy)
         lower_words = keep.tile([P, HALF], U32, name="lower_words", align_bytes=64)
         upper_words = keep.tile([P, HALF], U32, name="upper_words", tag="late_0", align_bytes=64)
+        a = PASSES - 1
         for s in ORDER:
+            for early in {3: (1,), 1: (0, 1)}.get(s, ()):
+                multiply(early, s)
             words = (lower_words, upper_words)[s // 2]
             quantize(a, s * PART, (s + 1) * PART, ends[s], words[:, s % 2 * PART : (s % 2 + 1) * PART])
             multiply(a, s)
@@ -169,7 +188,7 @@ def tile_picked_pool_lin_gelu_sub_e_kernel(tc, xT, w_words, w_scales, b, offs, o
         out_view = out.rearrange("(m p) v -> p m v", p=P)
         for s in ORDER:
             for m in range(M_TILES):
-                nc.scalar.activation(act[m][s][:], acc[m][s][:], GELU, bias=bias[:, m : m + 1])
+                nc.scalar.activation(act[m][s][:], acc[m][s], GELU, bias=bias[:, m : m + 1])
                 nc.vector.tensor_reduce(
                     out=pooled[:, m, s * PART // D : (s + 1) * PART // D],
                     in_=act[m][s][:].rearrange("p (v d) -> p v d", d=D),

@@ -116,6 +116,18 @@ def tile_picked_pool_lin_gelu_sub_e_kernel(tc, xT, w_words, w_scales, b, offs, o
                 in_=values.rearrange("p n j -> p (n j)"),
             )
 
+        def warm_up(words, first):
+            for i in range(WARM_UPS):
+                nc.tensor.matmul_mx(
+                    out=banks[1][1][0:WARM_ROWS, :],
+                    lhsT=words[:, 0:WARM_ROWS].bitcast(FP8X4),
+                    lhsT_scale=scales[1][:, first : first + WARM_ROWS],
+                    rhs=first_words[:].bitcast(FP8X4),
+                    rhs_scale=scales[0][:],
+                    start=True,
+                    stop=True,
+                )
+
         def gather(a, j):
             nc.vector.tensor_copy(grouped[a][:, :, j], plane(a, j).indirect(offsets[:]))
 
@@ -150,6 +162,7 @@ def tile_picked_pool_lin_gelu_sub_e_kernel(tc, xT, w_words, w_scales, b, offs, o
             else:
                 quantize(a, 0, PART, grouped[a][:, 0:PART, :], words[:, 0:PART])
                 quantize(a, HALF, S, grouped[a][:, HALF:S, :], words[:, HALF:S])
+                warm_up(words[:, HALF:S], HALF)
         a = PASSES - 1
         gather_pair(a)
         for s in range(PARTS):
@@ -160,16 +173,7 @@ def tile_picked_pool_lin_gelu_sub_e_kernel(tc, xT, w_words, w_scales, b, offs, o
         gather_late(2)
         held = keep.tile([P, PART], U32, name="held", tag="x_2_0", align_bytes=64)
         quantize(1, PART, HALF, grouped[1][:, PART:HALF, :], held[:])
-        for i in range(WARM_UPS):
-            nc.tensor.matmul_mx(
-                out=banks[1][1][0:WARM_ROWS, :],
-                lhsT=held[:, 0:WARM_ROWS].bitcast(FP8X4),
-                lhsT_scale=scales[1][:, PART : PART + WARM_ROWS],
-                rhs=first_words[:].bitcast(FP8X4),
-                rhs_scale=scales[0][:],
-                start=True,
-                stop=True,
-            )
+        warm_up(held[:], PART)
         for a, s in ((0, 0), (0, 2), (1, 0), (1, 2), (0, 3)):
             multiply(a, s)
         gather_late(3)

@@ -25,7 +25,7 @@ LOADS = (((0, 4),), ((0, 2), (2, 4)), ((0, 2), (2, 3), (3, 4)))
 PAIR = 2
 ORDER = (0, 2, 3, 1)
 SLICES = ((0, PART), (PART, HALF))
-WARM_UPS = 3
+WARM_UPS = 4
 WARM_ROWS = 32
 
 
@@ -85,9 +85,10 @@ def tile_picked_pool_lin_gelu_sub_e_kernel(tc, xT, w_words, w_scales, b, offs, o
 
         load_block(0, 0)
         nc.sync.dma_start(offsets[:], offs)
-        load_scales()
-        for a, i in ((1, 0), (1, 1), (2, 0), (2, 1), (2, 2)):
+        for a, i in ((1, 0), (1, 1), (2, 0), (2, 1)):
             load_block(a, i)
+        load_scales()
+        load_block(2, 2)
         for a in range(PASSES):
             load_weights(a)
         with nc.allow_non_contiguous_dma(reason="one bias value a partition"):
@@ -116,13 +117,13 @@ def tile_picked_pool_lin_gelu_sub_e_kernel(tc, xT, w_words, w_scales, b, offs, o
                 in_=values.rearrange("p n j -> p (n j)"),
             )
 
-        def warm_up(words, first):
+        def warm_up(words):
             for i in range(WARM_UPS):
                 nc.tensor.matmul_mx(
                     out=banks[1][1][0:WARM_ROWS, :],
                     lhsT=words[:, 0:WARM_ROWS].bitcast(FP8X4),
-                    lhsT_scale=scales[1][:, first : first + WARM_ROWS],
-                    rhs=first_words[:].bitcast(FP8X4),
+                    lhsT_scale=w_scale[:, 0, 0:WARM_ROWS],
+                    rhs=words.bitcast(FP8X4),
                     rhs_scale=scales[0][:],
                     start=True,
                     stop=True,
@@ -156,13 +157,9 @@ def tile_picked_pool_lin_gelu_sub_e_kernel(tc, xT, w_words, w_scales, b, offs, o
             for j in range(PAIR, PACK):
                 gather(a, j)
             words = keep.tile([P, S], U32, name=f"codes_{a}", align_bytes=64)
+            quantize(a, 0, S, grouped[a][:], words[:])
             if a == 0:
-                first_words = words
-                quantize(a, 0, S, grouped[a][:], words[:])
-            else:
-                quantize(a, 0, PART, grouped[a][:, 0:PART, :], words[:, 0:PART])
-                quantize(a, HALF, S, grouped[a][:, HALF:S, :], words[:, HALF:S])
-                warm_up(words[:, HALF:S], HALF)
+                warm_up(words[:])
         a = PASSES - 1
         gather_pair(a)
         for s in range(PARTS):
@@ -171,9 +168,6 @@ def tile_picked_pool_lin_gelu_sub_e_kernel(tc, xT, w_words, w_scales, b, offs, o
                 picked[a][:, :, s * PART : (s + 1) * PART].rearrange("p j n -> p n j"),
             )
         gather_late(2)
-        held = keep.tile([P, PART], U32, name="held", tag="x_2_0", align_bytes=64)
-        quantize(1, PART, HALF, grouped[1][:, PART:HALF, :], held[:])
-        warm_up(held[:], PART)
         for a, s in ((0, 0), (0, 2), (1, 0), (1, 2), (0, 3)):
             multiply(a, s)
         gather_late(3)

@@ -25,7 +25,8 @@ LOADS = (((0, 4),), ((0, 2), (2, 4)), ((0, 2), (2, 3), (3, 4)))
 PAIR = 2
 ORDER = (0, 2, 3, 1)
 SLICES = ((0, PART), (PART, HALF))
-WARM_UPS = 4
+WARM_UPS = 2
+BLOCK = 8
 WARM_ROWS = 32
 
 
@@ -38,7 +39,7 @@ def tile_picked_pool_lin_gelu_sub_e_kernel(tc, xT, w_words, w_scales, b, offs, o
         offsets = keep.tile([P, S // 16], U16, name="offsets")
         w_codes = [keep.tile([P, N], I32, name=f"w_codes_{a}", align_bytes=64) for a in range(PASSES)]
         w_scale = keep.tile([P, PASSES, N], U8, name="w_scale", align_bytes=64)
-        bias = keep.tile([P, M_TILES], F32, name="bias")
+        bias = keep.tile([P, M_TILES, BLOCK], F32, name="bias")
         warm = keep.tile([P, 1], F32, name="warm")
 
         blocks = [
@@ -92,7 +93,7 @@ def tile_picked_pool_lin_gelu_sub_e_kernel(tc, xT, w_words, w_scales, b, offs, o
         for a in range(PASSES):
             load_weights(a)
         with nc.allow_non_contiguous_dma(reason="one bias value a partition"):
-            nc.sync.dma_start(out=bias[:], in_=b.rearrange("(m p) o -> p (m o)", p=P))
+            nc.sync.dma_start(out=bias[:, :, 0:1], in_=b.rearrange("(m p) o -> p m o", p=P))
 
         def multiply(a, s):
             cols = slice(s * PART, (s + 1) * PART)
@@ -117,12 +118,12 @@ def tile_picked_pool_lin_gelu_sub_e_kernel(tc, xT, w_words, w_scales, b, offs, o
                 in_=values.rearrange("p n j -> p (n j)"),
             )
 
-        def warm_up(words):
+        def warm_up(held, held_scales, words):
             for i in range(WARM_UPS):
                 nc.tensor.matmul_mx(
                     out=banks[1][1][0:WARM_ROWS, :],
-                    lhsT=words[:, 0:WARM_ROWS].bitcast(FP8X4),
-                    lhsT_scale=w_scale[:, 0, 0:WARM_ROWS],
+                    lhsT=held[:, 0:WARM_ROWS].bitcast(FP8X4),
+                    lhsT_scale=held_scales[:, 0:WARM_ROWS],
                     rhs=words.bitcast(FP8X4),
                     rhs_scale=scales[0][:],
                     start=True,
@@ -157,9 +158,12 @@ def tile_picked_pool_lin_gelu_sub_e_kernel(tc, xT, w_words, w_scales, b, offs, o
             for j in range(PAIR, PACK):
                 gather(a, j)
             words = keep.tile([P, S], U32, name=f"codes_{a}", align_bytes=64)
-            quantize(a, 0, S, grouped[a][:], words[:])
             if a == 0:
-                warm_up(words[:])
+                first_words = words
+                quantize(a, 0, S, grouped[a][:], words[:])
+            else:
+                for first, last in ((0, PART), (HALF, S)):
+                    quantize(a, first, last, grouped[a][:, first:last, :], words[:, first:last])
         a = PASSES - 1
         gather_pair(a)
         for s in range(PARTS):
@@ -168,6 +172,9 @@ def tile_picked_pool_lin_gelu_sub_e_kernel(tc, xT, w_words, w_scales, b, offs, o
                 picked[a][:, :, s * PART : (s + 1) * PART].rearrange("p j n -> p n j"),
             )
         gather_late(2)
+        held = keep.tile([P, PART], U32, name="held_words", tag="x_2_2", align_bytes=64)
+        quantize(1, PART, HALF, grouped[1][:, PART:HALF, :], held[:])
+        warm_up(held[:], scales[1][:, PART:HALF], first_words[:])
         for a, s in ((0, 0), (0, 2), (1, 0), (1, 2), (0, 3)):
             multiply(a, s)
         gather_late(3)
@@ -186,7 +193,7 @@ def tile_picked_pool_lin_gelu_sub_e_kernel(tc, xT, w_words, w_scales, b, offs, o
         out_view = out.rearrange("(m p) v -> p m v", p=P)
         for s in ORDER:
             for m in range(M_TILES):
-                nc.scalar.activation(act[m][s][:], acc[m][s], GELU, bias=bias[:, m : m + 1])
+                nc.scalar.activation(act[m][s][:], acc[m][s], GELU, bias=bias[:, m, 0:1])
                 nc.vector.tensor_reduce(
                     out=pooled[:, m, s * PART // D : (s + 1) * PART // D],
                     in_=act[m][s][:].rearrange("p (v d) -> p v d", d=D),

@@ -130,9 +130,6 @@ def tile_picked_pool_lin_gelu_sub_e_kernel(tc, xT, w_words, w_scales, b, offs, o
                     stop=True,
                 )
 
-        def gather(a, j):
-            nc.vector.tensor_copy(grouped[a][:, :, j], plane(a, j).indirect(offsets[:]))
-
         def gather_pair(a):
             for j in range(PAIR):
                 nc.vector.tensor_copy(picked[a][:, j, :], plane(a, j).indirect(offsets[:]))
@@ -155,13 +152,17 @@ def tile_picked_pool_lin_gelu_sub_e_kernel(tc, xT, w_words, w_scales, b, offs, o
         for a in range(PASSES - 1):
             gather_pair(a)
             nc.scalar.copy(grouped[a][:, :, 0:PAIR], picked[a][:].rearrange("p j n -> p n j"))
-            for j in range(PAIR, PACK):
-                gather(a, j)
-            words = keep.tile([P, S], U32, name=f"codes_{a}", align_bytes=64)
-            if a == 0:
-                first_words = words
-                quantize(a, 0, S, grouped[a][:], words[:])
-            else:
+            if a == 1:
+                first_words = keep.tile([P, S], U32, name="codes_0", tag="x_1_0", align_bytes=64)
+                quantize(0, 0, S, grouped[0][:], first_words[:])
+            width = S // (a + 1)
+            for first in range(0, S, width):
+                second = keep.tile([P, PAIR, width], F32, name=f"second_{a}_{first}")
+                for j in range(PAIR):
+                    nc.vector.tensor_copy(second[:, j, :], plane(a, PAIR + j).indirect(offsets[:, first // 16 : (first + width) // 16]))
+                nc.scalar.copy(grouped[a][:, first : first + width, PAIR:PACK], second[:].rearrange("p j n -> p n j"))
+            if a == 1:
+                words = keep.tile([P, S], U32, name="codes_1", align_bytes=64)
                 for first, last in ((0, PART), (HALF, S)):
                     quantize(a, first, last, grouped[a][:, first:last, :], words[:, first:last])
         a = PASSES - 1

@@ -27,7 +27,7 @@ ORDER = (0, 2, 3, 1)
 SLICES = ((0, PART), (PART, HALF))
 WARM_UPS = 2
 BLOCK = 8
-WARM_ROWS = 32
+WARM_ROWS = 64
 
 
 def tile_picked_pool_lin_gelu_sub_e_kernel(tc, xT, w_words, w_scales, b, offs, out):
@@ -90,12 +90,13 @@ def tile_picked_pool_lin_gelu_sub_e_kernel(tc, xT, w_words, w_scales, b, offs, o
             load_block(a, i)
         load_scales()
         load_block(2, 2)
-        for a in range(PASSES):
-            load_weights(a)
+        load_weights(0)
+        load_weights(2)
+        load_weights(1)
         with nc.allow_non_contiguous_dma(reason="one bias value a partition"):
             nc.sync.dma_start(out=bias[:, :, 0:1], in_=b.rearrange("(m p) o -> p m o", p=P))
 
-        def multiply(a, s):
+        def multiply(a, s, start):
             cols = slice(s * PART, (s + 1) * PART)
             for m in range(M_TILES):
                 rows = slice(m * P, (m + 1) * P)
@@ -105,7 +106,7 @@ def tile_picked_pool_lin_gelu_sub_e_kernel(tc, xT, w_words, w_scales, b, offs, o
                     lhsT_scale=w_scale[:, a, rows],
                     rhs=codes[a, s].bitcast(FP8X4),
                     rhs_scale=scales[a][:, cols],
-                    start=(a == 0),
+                    start=start,
                     stop=(a == PASSES - 1),
                 )
 
@@ -176,8 +177,8 @@ def tile_picked_pool_lin_gelu_sub_e_kernel(tc, xT, w_words, w_scales, b, offs, o
         held = keep.tile([P, PART], U32, name="held_words", tag="x_2_2", align_bytes=64)
         quantize(1, PART, HALF, grouped[1][:, PART:HALF, :], held[:])
         warm_up(held[:], scales[1][:, PART:HALF], first_words[:])
-        for a, s in ((0, 0), (0, 2), (1, 0), (1, 2), (0, 3)):
-            multiply(a, s)
+        for s in ORDER[:-1]:
+            multiply(0, s, True)
         gather_late(3)
         for s in range(2):
             weave_late(s, nc.scalar.copy)
@@ -185,11 +186,12 @@ def tile_picked_pool_lin_gelu_sub_e_kernel(tc, xT, w_words, w_scales, b, offs, o
         upper_words = keep.tile([P, HALF], U32, name="upper_words", tag="late_0", align_bytes=64)
         a = PASSES - 1
         for s in ORDER:
-            for early in {3: (1,), 1: (0, 1)}.get(s, ()):
-                multiply(early, s)
+            multiply(1, s, s == ORDER[-1])
+            if s == ORDER[-1]:
+                multiply(0, s, False)
             words = (lower_words, upper_words)[s // 2]
             quantize(a, s * PART, (s + 1) * PART, ends[s], words[:, s % 2 * PART : (s % 2 + 1) * PART])
-            multiply(a, s)
+            multiply(a, s, False)
         pooled = keep.tile([P, M_TILES, S // D], F32, name="pooled", tag="ends_1", align_bytes=64)
         out_view = out.rearrange("(m p) v -> p m v", p=P)
         for s in ORDER:

@@ -26,6 +26,7 @@ PAIR = 2
 ORDER = (0, 2, 3, 1)
 SLICES = ((0, PART), (PART, HALF))
 WARM_UPS = 2
+EARLY = 640
 BLOCK = 8
 WARM_ROWS = 64
 
@@ -88,15 +89,17 @@ def tile_picked_pool_lin_gelu_sub_e_kernel(tc, xT, w_words, w_scales, b, offs, o
         nc.sync.dma_start(offsets[:], offs)
         for a, i in ((1, 0), (1, 1), (2, 0), (2, 1)):
             load_block(a, i)
+        last_plane = x_view[2, :, 3 * T : 4 * T]
+        nc.sync.dma_start(out=blocks[2][2][:, 0:EARLY], in_=last_plane[:, 0:EARLY])
         load_scales()
-        load_block(2, 2)
+        nc.sync.dma_start(out=blocks[2][2][:, EARLY:T], in_=last_plane[:, EARLY:T])
         load_weights(0)
         load_weights(2)
         load_weights(1)
         with nc.allow_non_contiguous_dma(reason="one bias value a partition"):
             nc.sync.dma_start(out=bias[:, :, 0:1], in_=b.rearrange("(m p) o -> p m o", p=P))
 
-        def multiply(a, s, start):
+        def multiply(a, s):
             cols = slice(s * PART, (s + 1) * PART)
             for m in range(M_TILES):
                 rows = slice(m * P, (m + 1) * P)
@@ -106,7 +109,7 @@ def tile_picked_pool_lin_gelu_sub_e_kernel(tc, xT, w_words, w_scales, b, offs, o
                     lhsT_scale=w_scale[:, a, rows],
                     rhs=codes[a, s].bitcast(FP8X4),
                     rhs_scale=scales[a][:, cols],
-                    start=start,
+                    start=(a == 0),
                     stop=(a == PASSES - 1),
                 )
 
@@ -164,7 +167,7 @@ def tile_picked_pool_lin_gelu_sub_e_kernel(tc, xT, w_words, w_scales, b, offs, o
                 nc.scalar.copy(grouped[a][:, first : first + width, PAIR:PACK], second[:].rearrange("p j n -> p n j"))
             if a == 1:
                 words = keep.tile([P, S], U32, name="codes_1", align_bytes=64)
-                for first, last in ((0, PART), (HALF, S)):
+                for first, last in ((0, HALF), (HALF, S)):
                     quantize(a, first, last, grouped[a][:, first:last, :], words[:, first:last])
         a = PASSES - 1
         gather_pair(a)
@@ -174,11 +177,9 @@ def tile_picked_pool_lin_gelu_sub_e_kernel(tc, xT, w_words, w_scales, b, offs, o
                 picked[a][:, :, s * PART : (s + 1) * PART].rearrange("p j n -> p n j"),
             )
         gather_late(2)
-        held = keep.tile([P, PART], U32, name="held_words", tag="x_2_2", align_bytes=64)
-        quantize(1, PART, HALF, grouped[1][:, PART:HALF, :], held[:])
-        warm_up(held[:], scales[1][:, PART:HALF], first_words[:])
-        for s in ORDER[:-1]:
-            multiply(0, s, True)
+        warm_up(first_words[:], w_scale[:, 0, :], first_words[:])
+        for s in ORDER:
+            multiply(0, s)
         gather_late(3)
         for s in range(2):
             weave_late(s, nc.scalar.copy)
@@ -186,12 +187,10 @@ def tile_picked_pool_lin_gelu_sub_e_kernel(tc, xT, w_words, w_scales, b, offs, o
         upper_words = keep.tile([P, HALF], U32, name="upper_words", tag="late_0", align_bytes=64)
         a = PASSES - 1
         for s in ORDER:
-            multiply(1, s, s == ORDER[-1])
-            if s == ORDER[-1]:
-                multiply(0, s, False)
+            multiply(1, s)
             words = (lower_words, upper_words)[s // 2]
             quantize(a, s * PART, (s + 1) * PART, ends[s], words[:, s % 2 * PART : (s % 2 + 1) * PART])
-            multiply(a, s, False)
+            multiply(a, s)
         pooled = keep.tile([P, M_TILES, S // D], F32, name="pooled", tag="ends_1", align_bytes=64)
         out_view = out.rearrange("(m p) v -> p m v", p=P)
         for s in ORDER:

@@ -21,12 +21,12 @@ M_TILES = N // P
 HALF = S // 2
 PART = 128
 PARTS = S // PART
-LOADS = (((0, 4),), ((0, 2), (2, 4)), ((0, 2), (2, 3), (3, 4)))
+LOADS = (((0, 4),), ((0, 2), (2, 4)), ((0, 2), (2, 4)))
 PAIR = 2
 ORDER = (0, 2, 3, 1)
 SLICES = ((0, PART), (PART, HALF))
 WARM_UPS = 2
-EARLY = 640
+EARLY = 512
 BLOCK = 8
 WARM_ROWS = 64
 
@@ -87,12 +87,12 @@ def tile_picked_pool_lin_gelu_sub_e_kernel(tc, xT, w_words, w_scales, b, offs, o
 
         load_block(0, 0)
         nc.sync.dma_start(offsets[:], offs)
-        for a, i in ((1, 0), (1, 1), (2, 0), (2, 1)):
+        for a, i in ((1, 0), (1, 1), (2, 0)):
             load_block(a, i)
-        last_plane = x_view[2, :, 3 * T : 4 * T]
-        nc.sync.dma_start(out=blocks[2][2][:, 0:EARLY], in_=last_plane[:, 0:EARLY])
+        last_block, last_rows = blocks[2][1], x_view[2, :, PAIR * T : PACK * T]
+        nc.sync.dma_start(out=last_block[:, T - EARLY :], in_=last_rows[:, T - EARLY :])
         load_scales()
-        nc.sync.dma_start(out=blocks[2][2][:, EARLY:T], in_=last_plane[:, EARLY:T])
+        nc.sync.dma_start(out=last_block[:, 0 : T - EARLY], in_=last_rows[:, 0 : T - EARLY])
         load_weights(0)
         load_weights(2)
         load_weights(1)
@@ -138,15 +138,6 @@ def tile_picked_pool_lin_gelu_sub_e_kernel(tc, xT, w_words, w_scales, b, offs, o
             for j in range(PAIR):
                 nc.vector.tensor_copy(picked[a][:, j, :], plane(a, j).indirect(offsets[:]))
 
-        def gather_late(j):
-            for (first, last), tile in zip(SLICES, late):
-                width = last - first
-                nc.vector.tensor_copy(
-                    tile[:, (j - PAIR) * width : (j - PAIR + 1) * width],
-                    blocks[PASSES - 1][j - 1][:].indirect(offsets[:, first // 16 : last // 16]),
-                )
-            nc.vector.tensor_copy(upper[:, :, j], plane(PASSES - 1, j).indirect(offsets[:, HALF // 16 : S // 16]))
-
         def weave_late(s, copy):
             for (first, last), tile in zip(SLICES, late):
                 if first <= s * PART < last:
@@ -176,11 +167,17 @@ def tile_picked_pool_lin_gelu_sub_e_kernel(tc, xT, w_words, w_scales, b, offs, o
                 ends[s][:, :, 0:PAIR],
                 picked[a][:, :, s * PART : (s + 1) * PART].rearrange("p j n -> p n j"),
             )
-        gather_late(2)
+        staged = keep.tile([P, HALF], F32, name="staged")
+        nc.vector.tensor_copy(staged[:], plane(a, 3).indirect(offsets[:, 0 : HALF // 16]))
+        nc.vector.tensor_copy(upper[:, :, 3], plane(a, 3).indirect(offsets[:, HALF // 16 : S // 16]))
+        for (first, last), tile in zip(SLICES, late):
+            nc.scalar.copy(tile[:, PART:HALF], staged[:, first:last])
         warm_up(first_words[:], w_scale[:, 0, :], first_words[:])
         for s in ORDER:
             multiply(0, s)
-        gather_late(3)
+        for (first, last), tile in zip(SLICES, late):
+            nc.vector.tensor_copy(tile[:, 0:PART], last_block[:].indirect(offsets[:, first // 16 : last // 16]))
+        nc.vector.tensor_copy(upper[:, :, 2], plane(a, 2).indirect(offsets[:, HALF // 16 : S // 16]))
         for s in range(2):
             weave_late(s, nc.scalar.copy)
         lower_words = keep.tile([P, HALF], U32, name="lower_words", align_bytes=64)

@@ -61,7 +61,6 @@ def tile_picked_pool_lin_gelu_sub_e_kernel(tc, xT, w_words, w_scales, b, offs, o
 
         nc.vector.memset(w_scale[:].bitcast(I32), 0)
         nc.vector.memset(warm[:], 0.0)
-        nc.scalar.activation(warm[:], warm[:], GELU)
 
         x_view = xT.rearrange("(a p j) t -> a p (j t)", p=P, j=PACK)
         w_view = w_words.rearrange("a p m r -> a p (m r)").bitcast(I32)
@@ -78,20 +77,22 @@ def tile_picked_pool_lin_gelu_sub_e_kernel(tc, xT, w_words, w_scales, b, offs, o
         def load_weights(a):
             nc.sync.dma_start(out=w_codes[a][:], in_=w_view[a])
 
-        def load_scales():
-            for q in range(4):
-                nc.sync.dma_start(
+        def load_scales(queue, quadrants):
+            for q in quadrants:
+                queue.dma_start(
                     out=w_scale[32 * q : 32 * q + 4, :, :].bitcast(I32),
                     in_=w_scales[:, 4 * q : 4 * q + 4, :].rearrange("a r m -> r a m").bitcast(I32),
                 )
 
         load_block(0, 0)
+        load_scales(nc.scalar, range(3))
+        nc.scalar.activation(warm[:], warm[:], GELU)
         nc.sync.dma_start(offsets[:], offs)
         for a, i in ((1, 0), (1, 1), (2, 0)):
             load_block(a, i)
         last_block, last_rows = blocks[2][1], x_view[2, :, PAIR * T : PACK * T]
         nc.sync.dma_start(out=last_block[:, T - EARLY :], in_=last_rows[:, T - EARLY :])
-        load_scales()
+        load_scales(nc.sync, [3])
         nc.sync.dma_start(out=last_block[:, 0 : T - EARLY], in_=last_rows[:, 0 : T - EARLY])
         load_weights(0)
         load_weights(2)

@@ -21,13 +21,12 @@ M_TILES = N // P
 HALF = S // 2
 PART = 128
 PARTS = S // PART
-LOADS = (((0, 4),), ((0, 2), (2, 4)), ((0, 2), (2, 4)))
+LOADS = (((0, 4),), ((0, 2), (2, 4)), ((0, 2), (3, 4), (2, 3)))
 PAIR = 2
 ORDER = (0, 2, 3, 1)
 SLICES = ((0, PART), (PART, HALF))
 WARM_UPS = 2
-EARLY = 512
-BLOCK = 8
+SQUARE = 32
 WARM_ROWS = 64
 
 
@@ -40,7 +39,7 @@ def tile_picked_pool_lin_gelu_sub_e_kernel(tc, xT, w_words, w_scales, b, offs, o
         offsets = keep.tile([P, S // 16], U16, name="offsets")
         w_codes = [keep.tile([P, N], I32, name=f"w_codes_{a}", align_bytes=64) for a in range(PASSES)]
         w_scale = keep.tile([P, PASSES, N], U8, name="w_scale", align_bytes=64)
-        bias = keep.tile([P, M_TILES, BLOCK], F32, name="bias")
+        bias_rows = keep.tile([P, M_TILES, SQUARE], F32, name="bias_rows", align_bytes=64)
         warm = keep.tile([P, 1], F32, name="warm")
 
         blocks = [
@@ -60,6 +59,7 @@ def tile_picked_pool_lin_gelu_sub_e_kernel(tc, xT, w_words, w_scales, b, offs, o
         act = [[keep.tile([P, PART], F32, name=f"act_{m}_{s}") for s in range(PARTS)] for m in range(M_TILES)]
 
         nc.vector.memset(w_scale[:].bitcast(I32), 0)
+        nc.vector.memset(bias_rows[:], 0.0)
         nc.vector.memset(warm[:], 0.0)
 
         x_view = xT.rearrange("(a p j) t -> a p (j t)", p=P, j=PACK)
@@ -85,20 +85,18 @@ def tile_picked_pool_lin_gelu_sub_e_kernel(tc, xT, w_words, w_scales, b, offs, o
                 )
 
         load_block(0, 0)
-        load_scales(nc.scalar, range(3))
+        load_scales(nc.scalar, range(4))
+        nc.scalar.dma_start(
+            out=bias_rows[0:P:SQUARE, :, :],
+            in_=b.rearrange("(m q i) o -> q m (i o)", m=M_TILES, i=SQUARE),
+        )
         nc.scalar.activation(warm[:], warm[:], GELU)
         nc.sync.dma_start(offsets[:], offs)
-        for a, i in ((1, 0), (1, 1), (2, 0)):
+        for a, i in ((1, 0), (1, 1), (2, 0), (2, 1), (2, 2)):
             load_block(a, i)
-        last_block, last_rows = blocks[2][1], x_view[2, :, PAIR * T : PACK * T]
-        nc.sync.dma_start(out=last_block[:, T - EARLY :], in_=last_rows[:, T - EARLY :])
-        load_scales(nc.sync, [3])
-        nc.sync.dma_start(out=last_block[:, 0 : T - EARLY], in_=last_rows[:, 0 : T - EARLY])
         load_weights(0)
         load_weights(2)
         load_weights(1)
-        with nc.allow_non_contiguous_dma(reason="one bias value a partition"):
-            nc.sync.dma_start(out=bias[:, :, 0:1], in_=b.rearrange("(m p) o -> p m o", p=P))
 
         def multiply(a, s):
             cols = slice(s * PART, (s + 1) * PART)
@@ -158,26 +156,28 @@ def tile_picked_pool_lin_gelu_sub_e_kernel(tc, xT, w_words, w_scales, b, offs, o
                     nc.vector.tensor_copy(second[:, j, :], plane(a, PAIR + j).indirect(offsets[:, first // 16 : (first + width) // 16]))
                 nc.scalar.copy(grouped[a][:, first : first + width, PAIR:PACK], second[:].rearrange("p j n -> p n j"))
             if a == 1:
-                words = keep.tile([P, S], U32, name="codes_1", align_bytes=64)
-                for first, last in ((0, HALF), (HALF, S)):
-                    quantize(a, first, last, grouped[a][:, first:last, :], words[:, first:last])
+                words = keep.tile([P, HALF], U32, name="codes_1", align_bytes=64)
+                quantize(a, 0, HALF, grouped[a][:, 0:HALF, :], words[:])
+        bias = keep.tile([P, M_TILES, SQUARE], F32, name="bias", tag="x_1_2", align_bytes=64)
+        for m in range(M_TILES):
+            nc.vector.transpose(bias[:, m, :], bias_rows[:, m, :])
         a = PASSES - 1
         gather_pair(a)
+        held_words = keep.tile([P, HALF], U32, name="codes_1_held", tag="x_2_0", align_bytes=64)
+        quantize(1, HALF, S, grouped[1][:, HALF:S, :], held_words[:])
         for s in range(PARTS):
             nc.scalar.copy(
                 ends[s][:, :, 0:PAIR],
                 picked[a][:, :, s * PART : (s + 1) * PART].rearrange("p j n -> p n j"),
             )
-        staged = keep.tile([P, HALF], F32, name="staged")
-        nc.vector.tensor_copy(staged[:], plane(a, 3).indirect(offsets[:, 0 : HALF // 16]))
-        nc.vector.tensor_copy(upper[:, :, 3], plane(a, 3).indirect(offsets[:, HALF // 16 : S // 16]))
         for (first, last), tile in zip(SLICES, late):
-            nc.scalar.copy(tile[:, PART:HALF], staged[:, first:last])
-        warm_up(first_words[:], w_scale[:, 0, :], first_words[:])
+            nc.vector.tensor_copy(tile[:, PART:HALF], plane(a, 3).indirect(offsets[:, first // 16 : last // 16]))
+        nc.vector.tensor_copy(upper[:, :, 3], plane(a, 3).indirect(offsets[:, HALF // 16 : S // 16]))
+        warm_up(held_words[:], scales[1][:, HALF:S], first_words[:])
         for s in ORDER:
             multiply(0, s)
         for (first, last), tile in zip(SLICES, late):
-            nc.vector.tensor_copy(tile[:, 0:PART], last_block[:].indirect(offsets[:, first // 16 : last // 16]))
+            nc.vector.tensor_copy(tile[:, 0:PART], plane(a, 2).indirect(offsets[:, first // 16 : last // 16]))
         nc.vector.tensor_copy(upper[:, :, 2], plane(a, 2).indirect(offsets[:, HALF // 16 : S // 16]))
         for s in range(2):
             weave_late(s, nc.scalar.copy)

@@ -26,7 +26,7 @@ PAIR = 2
 ORDER = (0, 2, 3, 1)
 SLICES = ((0, PART), (PART, HALF))
 WARM_UPS = 2
-SQUARE = 32
+BLOCK = 8
 WARM_ROWS = 64
 
 
@@ -39,7 +39,7 @@ def tile_picked_pool_lin_gelu_sub_e_kernel(tc, xT, w_words, w_scales, b, offs, o
         offsets = keep.tile([P, S // 16], U16, name="offsets")
         w_codes = [keep.tile([P, N], I32, name=f"w_codes_{a}", align_bytes=64) for a in range(PASSES)]
         w_scale = keep.tile([P, PASSES, N], U8, name="w_scale", align_bytes=64)
-        bias_rows = keep.tile([P, M_TILES, SQUARE], F32, name="bias_rows", align_bytes=64)
+        bias = keep.tile([P, M_TILES, BLOCK], F32, name="bias")
         warm = keep.tile([P, 1], F32, name="warm")
 
         blocks = [
@@ -58,9 +58,8 @@ def tile_picked_pool_lin_gelu_sub_e_kernel(tc, xT, w_words, w_scales, b, offs, o
         acc = [[bank[:, 0:PART] for bank in row] for row in banks]
         act = [[keep.tile([P, PART], F32, name=f"act_{m}_{s}") for s in range(PARTS)] for m in range(M_TILES)]
 
-        nc.vector.memset(w_scale[:].bitcast(I32), 0)
-        nc.vector.memset(bias_rows[:], 0.0)
-        nc.vector.memset(warm[:], 0.0)
+        nc.gpsimd.memset(w_scale[:].bitcast(I32), 0)
+        nc.gpsimd.memset(warm[:], 0.0)
 
         x_view = xT.rearrange("(a p j) t -> a p (j t)", p=P, j=PACK)
         w_view = w_words.rearrange("a p m r -> a p (m r)").bitcast(I32)
@@ -86,10 +85,6 @@ def tile_picked_pool_lin_gelu_sub_e_kernel(tc, xT, w_words, w_scales, b, offs, o
 
         load_block(0, 0)
         load_scales(nc.scalar, range(4))
-        nc.scalar.dma_start(
-            out=bias_rows[0:P:SQUARE, :, :],
-            in_=b.rearrange("(m q i) o -> q m (i o)", m=M_TILES, i=SQUARE),
-        )
         nc.scalar.activation(warm[:], warm[:], GELU)
         nc.sync.dma_start(offsets[:], offs)
         for a, i in ((1, 0), (1, 1), (2, 0), (2, 1), (2, 2)):
@@ -97,6 +92,8 @@ def tile_picked_pool_lin_gelu_sub_e_kernel(tc, xT, w_words, w_scales, b, offs, o
         load_weights(0)
         load_weights(2)
         load_weights(1)
+        with nc.allow_non_contiguous_dma(reason="one bias value a partition"):
+            nc.sync.dma_start(out=bias[:, :, 0:1], in_=b.rearrange("(m p) o -> p m o", p=P))
 
         def multiply(a, s):
             cols = slice(s * PART, (s + 1) * PART)
@@ -158,9 +155,6 @@ def tile_picked_pool_lin_gelu_sub_e_kernel(tc, xT, w_words, w_scales, b, offs, o
             if a == 1:
                 words = keep.tile([P, HALF], U32, name="codes_1", align_bytes=64)
                 quantize(a, 0, HALF, grouped[a][:, 0:HALF, :], words[:])
-        bias = keep.tile([P, M_TILES, SQUARE], F32, name="bias", tag="x_1_2", align_bytes=64)
-        for m in range(M_TILES):
-            nc.vector.transpose(bias[:, m, :], bias_rows[:, m, :])
         a = PASSES - 1
         gather_pair(a)
         held_words = keep.tile([P, HALF], U32, name="codes_1_held", tag="x_2_0", align_bytes=64)

@@ -13,27 +13,29 @@ U16 = mybir.dt.uint16
 U8 = mybir.dt.uint8
 FP8X4 = mybir.dt.float8_e4m3fn_x4
 GELU = mybir.ActivationFunctionType.Gelu_apprx_tanh
+COPY = mybir.ActivationFunctionType.Copy
 
 P = 128
 PACK = 4
 PASSES = K // (P * PACK)
+LAST = PASSES - 1
 M_TILES = N // P
 HALF = S // 2
 PART = 128
 PARTS = S // PART
-LOADS = (((0, 4),), ((0, 2), (2, 4)), ((0, 2), (3, 4), (2, 3)))
 PAIR = 2
-ORDER = (0, 2, 3, 1)
-SLICES = ((0, PART), (PART, HALF))
+LOADS = (((0, 4),), ((0, 2), (2, 4)), ((0, 2), (3, 4), (2, 3)))
+PASS_ORDER = (1, 0, 2)
 WARM_UPS = 2
+WARM_ROWS = 32
 BLOCK = 8
-WARM_ROWS = 64
 
 
 def tile_picked_pool_lin_gelu_sub_e_kernel(tc, xT, w_words, w_scales, b, offs, out):
     nc = tc.nc
     with ExitStack() as ctx:
         keep = ctx.enter_context(tc.tile_pool(name="keep", bufs=1))
+        shared = ctx.enter_context(tc.tile_pool(name="shared", bufs=1))
         psum = ctx.enter_context(tc.psum_pool(name="psum", bufs=1))
 
         offsets = keep.tile([P, S // 16], U16, name="offsets")
@@ -41,22 +43,20 @@ def tile_picked_pool_lin_gelu_sub_e_kernel(tc, xT, w_words, w_scales, b, offs, o
         w_scale = keep.tile([P, PASSES, N], U8, name="w_scale", align_bytes=64)
         bias = keep.tile([P, M_TILES, BLOCK], F32, name="bias")
         warm = keep.tile([P, 1], F32, name="warm")
-
         blocks = [
             [keep.tile([P, (last - first) * T], F32, name=f"x_{a}_{first}", tag=f"x_{a}_{first}", align_bytes=64) for first, last in LOADS[a]]
             for a in range(PASSES)
         ]
-        grouped = [keep.tile([P, S, PACK], BF16, name=f"grouped_{a}", align_bytes=64) for a in range(PASSES - 1)]
-        picked = [keep.tile([P, PAIR, S], F32, name=f"picked_{a}") for a in range(PASSES)]
-        late = [keep.tile([P, PAIR * (last - first)], BF16, name=f"late_{first}", tag=f"late_{first}", align_bytes=64) for first, last in SLICES]
-        ends = [keep.tile([P, PART, PACK], BF16, name=f"ends_{s}", tag=f"ends_{s}", align_bytes=64)[:] for s in range(2)]
-        upper = keep.tile([P, HALF, PACK], BF16, name="upper", align_bytes=64)
-        ends = ends + [upper[:, s * PART : (s + 1) * PART, :] for s in range(2)]
-        codes = {}
+        grouped = [
+            keep.tile([P, S, PACK], BF16, name="grouped_0", align_bytes=64),
+            shared.tile([P, S, PACK], BF16, name="grouped_1", align_bytes=64, offset=0),
+        ]
+        ends = [keep.tile([P, PART, PACK], BF16, name=f"ends_{s}", align_bytes=64) for s in range(PARTS)]
         scales = [keep.tile([P, S], U8, name=f"scales_{a}", align_bytes=64) for a in range(PASSES)]
         banks = [[psum.tile([P, S], F32, name=f"acc_{m}_{s}") for s in range(PARTS)] for m in range(M_TILES)]
-        acc = [[bank[:, 0:PART] for bank in row] for row in banks]
         act = [[keep.tile([P, PART], F32, name=f"act_{m}_{s}") for s in range(PARTS)] for m in range(M_TILES)]
+        pooled = keep.tile([P, M_TILES, S // D], F32, name="pooled", align_bytes=64)
+        codes = {}
 
         nc.gpsimd.memset(w_scale[:].bitcast(I32), 0)
         nc.gpsimd.memset(warm[:], 0.0)
@@ -68,46 +68,28 @@ def tile_picked_pool_lin_gelu_sub_e_kernel(tc, xT, w_words, w_scales, b, offs, o
             first, last = LOADS[a][i]
             nc.sync.dma_start(out=blocks[a][i][:], in_=x_view[a, :, first * T : last * T])
 
-        def plane(a, j):
-            for (first, last), block in zip(LOADS[a], blocks[a]):
-                if first <= j < last:
-                    return block[:, (j - first) * T : (j - first + 1) * T]
-
-        def load_weights(a):
-            nc.sync.dma_start(out=w_codes[a][:], in_=w_view[a])
-
-        def load_scales(queue, quadrants):
-            for q in quadrants:
-                queue.dma_start(
-                    out=w_scale[32 * q : 32 * q + 4, :, :].bitcast(I32),
-                    in_=w_scales[:, 4 * q : 4 * q + 4, :].rearrange("a r m -> r a m").bitcast(I32),
-                )
-
         load_block(0, 0)
-        load_scales(nc.scalar, range(4))
+        for q in range(4):
+            nc.scalar.dma_start(
+                out=w_scale[32 * q : 32 * q + 4, :, :].bitcast(I32),
+                in_=w_scales[:, 4 * q : 4 * q + 4, :].rearrange("a r m -> r a m").bitcast(I32),
+            )
         nc.scalar.activation(warm[:], warm[:], GELU)
         nc.sync.dma_start(offsets[:], offs)
         for a, i in ((1, 0), (1, 1), (2, 0), (2, 1), (2, 2)):
             load_block(a, i)
-        load_weights(0)
-        load_weights(2)
-        load_weights(1)
+        for a in (1, 2, 0):
+            nc.sync.dma_start(out=w_codes[a][:], in_=w_view[a])
         with nc.allow_non_contiguous_dma(reason="one bias value a partition"):
             nc.sync.dma_start(out=bias[:, :, 0:1], in_=b.rearrange("(m p) o -> p m o", p=P))
 
-        def multiply(a, s):
-            cols = slice(s * PART, (s + 1) * PART)
-            for m in range(M_TILES):
-                rows = slice(m * P, (m + 1) * P)
-                nc.tensor.matmul_mx(
-                    out=acc[m][s],
-                    lhsT=w_codes[a][:, rows].bitcast(FP8X4),
-                    lhsT_scale=w_scale[:, a, rows],
-                    rhs=codes[a, s].bitcast(FP8X4),
-                    rhs_scale=scales[a][:, cols],
-                    start=(a == 0),
-                    stop=(a == PASSES - 1),
-                )
+        def picked_of(a, j, first, last):
+            for (low, high), block in zip(LOADS[a], blocks[a]):
+                if low <= j < high:
+                    return block[:, (j - low) * T : (j - low + 1) * T].indirect(offsets[:, first // 16 : last // 16])
+
+        def scalar_gather(dst, src):
+            nc.scalar.activation(dst, src, COPY)
 
         def quantize(a, first, last, values, words):
             for s in range(first // PART, last // PART):
@@ -118,80 +100,87 @@ def tile_picked_pool_lin_gelu_sub_e_kernel(tc, xT, w_words, w_scales, b, offs, o
                 in_=values.rearrange("p n j -> p (n j)"),
             )
 
-        def warm_up(held, held_scales, words):
-            for i in range(WARM_UPS):
+        def multiply(a, s):
+            cols = slice(s * PART, (s + 1) * PART)
+            for m in range(M_TILES):
+                rows = slice(m * P, (m + 1) * P)
                 nc.tensor.matmul_mx(
-                    out=banks[1][1][0:WARM_ROWS, :],
-                    lhsT=held[:, 0:WARM_ROWS].bitcast(FP8X4),
-                    lhsT_scale=held_scales[:, 0:WARM_ROWS],
-                    rhs=words.bitcast(FP8X4),
-                    rhs_scale=scales[0][:],
-                    start=True,
-                    stop=True,
+                    out=banks[m][s][:, 0:PART],
+                    lhsT=w_codes[a][:, rows].bitcast(FP8X4),
+                    lhsT_scale=w_scale[:, a, rows],
+                    rhs=codes[a, s].bitcast(FP8X4),
+                    rhs_scale=scales[a][:, cols],
+                    start=(a == PASS_ORDER[0]),
+                    stop=(a == LAST),
                 )
 
-        def gather_pair(a):
-            for j in range(PAIR):
-                nc.vector.tensor_copy(picked[a][:, j, :], plane(a, j).indirect(offsets[:]))
+        def pair_of_planes(a, u, engines, tag):
+            pair = keep.tile([P, PAIR, S], F32, name=f"pair_{a}_{u}", tag=tag, align_bytes=64)
+            for e, gather in enumerate(engines):
+                gather(pair[:, e, :], picked_of(a, PAIR * u + e, 0, S))
+            return pair
 
-        def weave_late(s, copy):
-            for (first, last), tile in zip(SLICES, late):
-                if first <= s * PART < last:
-                    cols = slice(s * PART - first, (s + 1) * PART - first)
-                    copy(ends[s][:, :, PAIR:PACK], tile[:].rearrange("p (j n) -> p n j", j=PAIR)[:, cols, :])
+        both_vector = (nc.vector.tensor_copy, nc.vector.tensor_copy)
+        for a in range(LAST):
+            for u in range(PAIR):
+                pair = pair_of_planes(a, u, both_vector, f"pair_{a}_{u}")
+                nc.scalar.copy(grouped[a][:, :, PAIR * u : PAIR * (u + 1)], pair[:].rearrange("p e n -> p n e"))
+        first_words = keep.tile([P, S], U32, name="first_words", tag="x_1_0", align_bytes=64)
+        quantize(0, 0, S, grouped[0][:], first_words[:])
 
-        for a in range(PASSES - 1):
-            gather_pair(a)
-            nc.scalar.copy(grouped[a][:, :, 0:PAIR], picked[a][:].rearrange("p j n -> p n j"))
-            if a == 1:
-                first_words = keep.tile([P, S], U32, name="codes_0", tag="x_1_0", align_bytes=64)
-                quantize(0, 0, S, grouped[0][:], first_words[:])
-            width = S // (a + 1)
-            for first in range(0, S, width):
-                second = keep.tile([P, PAIR, width], F32, name=f"second_{a}_{first}")
-                for j in range(PAIR):
-                    nc.vector.tensor_copy(second[:, j, :], plane(a, PAIR + j).indirect(offsets[:, first // 16 : (first + width) // 16]))
-                nc.scalar.copy(grouped[a][:, first : first + width, PAIR:PACK], second[:].rearrange("p j n -> p n j"))
-            if a == 1:
-                words = keep.tile([P, HALF], U32, name="codes_1", align_bytes=64)
-                quantize(a, 0, HALF, grouped[a][:, 0:HALF, :], words[:])
-        a = PASSES - 1
-        gather_pair(a)
-        held_words = keep.tile([P, HALF], U32, name="codes_1_held", tag="x_2_0", align_bytes=64)
-        quantize(1, HALF, S, grouped[1][:, HALF:S, :], held_words[:])
+        pair = pair_of_planes(LAST, 0, (nc.vector.tensor_copy, scalar_gather), "last_pair")
         for s in range(PARTS):
-            nc.scalar.copy(
-                ends[s][:, :, 0:PAIR],
-                picked[a][:, :, s * PART : (s + 1) * PART].rearrange("p j n -> p n j"),
+            copy = nc.vector.tensor_copy if s < 2 else nc.scalar.copy
+            copy(ends[s][:, :, 0:PAIR], pair[:, :, s * PART : (s + 1) * PART].rearrange("p e n -> p n e"))
+        held_words = keep.tile([P, S], U32, name="held_words", tag="x_2_0", align_bytes=64)
+        quantize(1, 0, S, grouped[1][:], held_words[:])
+        late = [
+            shared.tile([P, PAIR * PART], BF16, name=f"late_{s}", align_bytes=64, offset=s * PAIR * PART * 2) for s in range(PARTS)
+        ]
+        for s in range(PARTS):
+            gather = nc.vector.tensor_copy if s < 2 else scalar_gather
+            gather(late[s][:, PART : PAIR * PART], picked_of(LAST, 3, s * PART, (s + 1) * PART))
+        for i in range(WARM_UPS):
+            nc.tensor.matmul_mx(
+                out=banks[0][0][0:WARM_ROWS, :],
+                lhsT=held_words[:, 0:WARM_ROWS].bitcast(FP8X4),
+                lhsT_scale=scales[1][:, 0:WARM_ROWS],
+                rhs=held_words[:].bitcast(FP8X4),
+                rhs_scale=scales[1][:],
+                start=True,
+                stop=True,
             )
-        for (first, last), tile in zip(SLICES, late):
-            nc.vector.tensor_copy(tile[:, PART:HALF], plane(a, 3).indirect(offsets[:, first // 16 : last // 16]))
-        nc.vector.tensor_copy(upper[:, :, 3], plane(a, 3).indirect(offsets[:, HALF // 16 : S // 16]))
-        warm_up(held_words[:], scales[1][:, HALF:S], first_words[:])
-        for s in ORDER:
-            multiply(0, s)
-        for (first, last), tile in zip(SLICES, late):
-            nc.vector.tensor_copy(tile[:, 0:PART], plane(a, 2).indirect(offsets[:, first // 16 : last // 16]))
-        nc.vector.tensor_copy(upper[:, :, 2], plane(a, 2).indirect(offsets[:, HALF // 16 : S // 16]))
-        for s in range(2):
-            weave_late(s, nc.scalar.copy)
-        lower_words = keep.tile([P, HALF], U32, name="lower_words", align_bytes=64)
-        upper_words = keep.tile([P, HALF], U32, name="upper_words", tag="late_0", align_bytes=64)
-        a = PASSES - 1
-        for s in ORDER:
+        for s in range(PARTS):
             multiply(1, s)
-            words = (lower_words, upper_words)[s // 2]
-            quantize(a, s * PART, (s + 1) * PART, ends[s], words[:, s % 2 * PART : (s % 2 + 1) * PART])
-            multiply(a, s)
-        pooled = keep.tile([P, M_TILES, S // D], F32, name="pooled", tag="ends_1", align_bytes=64)
-        out_view = out.rearrange("(m p) v -> p m v", p=P)
-        for s in ORDER:
+
+        nc.vector.tensor_copy(late[0][:, 0 : PART // 2], picked_of(LAST, 2, 0, PART // 2))
+        scalar_gather(late[0][:, PART // 2 : PART], picked_of(LAST, 2, PART // 2, PART))
+        for s in range(1, PARTS):
+            gather = nc.vector.tensor_copy if s < 2 else scalar_gather
+            gather(late[s][:, 0:PART], picked_of(LAST, 2, s * PART, (s + 1) * PART))
+
+        last_words = [keep.tile([P, PART], U32, name=f"last_words_{s}", align_bytes=64) for s in range(PARTS)]
+
+        def weave(s, copy):
+            copy(ends[s][:, :, PAIR:PACK], late[s][:].rearrange("p (e n) -> p n e", e=PAIR))
+
+        def close(s):
+            quantize(LAST, s * PART, (s + 1) * PART, ends[s][:], last_words[s][:])
+            multiply(0, s)
+            multiply(LAST, s)
+
+        for s in range(PARTS):
+            weave(s, nc.vector.tensor_copy if s < 2 else nc.scalar.copy)
+        for s in range(PARTS):
+            close(s)
+
+        for s in range(PARTS):
             for m in range(M_TILES):
-                nc.scalar.activation(act[m][s][:], acc[m][s], GELU, bias=bias[:, m, 0:1])
+                nc.scalar.activation(act[m][s][:], banks[m][s][:, 0:PART], GELU, bias=bias[:, m, 0:1])
                 nc.vector.tensor_reduce(
                     out=pooled[:, m, s * PART // D : (s + 1) * PART // D],
                     in_=act[m][s][:].rearrange("p (v d) -> p v d", d=D),
                     op=mybir.AluOpType.max,
                     axis=mybir.AxisListType.X,
                 )
-        nc.sync.dma_start(out=out_view, in_=pooled[:])
+        nc.sync.dma_start(out=out.rearrange("(m p) v -> p m v", p=P), in_=pooled[:])

@@ -174,13 +174,20 @@ def tile_picked_pool_lin_gelu_sub_e_kernel(tc, xT, w_words, w_scales, b, offs, o
         for s in range(PARTS):
             close(s)
 
+        def finish(m, s, first, last):
+            nc.scalar.activation(act[m][s][:, first:last], banks[m][s][:, first:last], GELU, bias=bias[:, m, 0:1])
+            nc.vector.tensor_reduce(
+                out=pooled[:, m, (s * PART + first) // D : (s * PART + last) // D],
+                in_=act[m][s][:, first:last].rearrange("p (v d) -> p v d", d=D),
+                op=mybir.AluOpType.max,
+                axis=mybir.AxisListType.X,
+            )
+
         for s in range(PARTS):
             for m in range(M_TILES):
-                nc.scalar.activation(act[m][s][:], banks[m][s][:, 0:PART], GELU, bias=bias[:, m, 0:1])
-                nc.vector.tensor_reduce(
-                    out=pooled[:, m, s * PART // D : (s + 1) * PART // D],
-                    in_=act[m][s][:].rearrange("p (v d) -> p v d", d=D),
-                    op=mybir.AluOpType.max,
-                    axis=mybir.AxisListType.X,
-                )
+                if (s, m) == (PARTS - 1, M_TILES - 1):
+                    finish(m, s, 0, PART // 2)
+                    finish(m, s, PART // 2, PART)
+                else:
+                    finish(m, s, 0, PART)
         nc.sync.dma_start(out=out.rearrange("(m p) v -> p m v", p=P), in_=pooled[:])

@@ -28,6 +28,7 @@ LOADS = (((0, 4),), ((0, 2), (2, 4)), ((0, 2), (3, 4), (2, 3)))
 PASS_ORDER = (1, 0, 2)
 WARM_UPS = 2
 WARM_ROWS = 32
+LOAD_ALIGN = 256
 BLOCK = 8
 
 
@@ -39,12 +40,12 @@ def tile_picked_pool_lin_gelu_sub_e_kernel(tc, xT, w_words, w_scales, b, offs, o
         psum = ctx.enter_context(tc.psum_pool(name="psum", bufs=1))
 
         offsets = keep.tile([P, S // 16], U16, name="offsets")
-        w_codes = [keep.tile([P, N], I32, name=f"w_codes_{a}", align_bytes=64) for a in range(PASSES)]
+        w_codes = [keep.tile([P, N], I32, name=f"w_codes_{a}", align_bytes=LOAD_ALIGN) for a in range(PASSES)]
         w_scale = keep.tile([P, PASSES, N], U8, name="w_scale", align_bytes=64)
         bias = keep.tile([P, M_TILES, BLOCK], F32, name="bias")
         warm = keep.tile([P, 1], F32, name="warm")
         blocks = [
-            [keep.tile([P, (last - first) * T], F32, name=f"x_{a}_{first}", tag=f"x_{a}_{first}", align_bytes=64) for first, last in LOADS[a]]
+            [keep.tile([P, (last - first) * T], F32, name=f"x_{a}_{first}", tag=f"x_{a}_{first}", align_bytes=LOAD_ALIGN) for first, last in LOADS[a]]
             for a in range(PASSES)
         ]
         grouped = [
@@ -125,21 +126,20 @@ def tile_picked_pool_lin_gelu_sub_e_kernel(tc, xT, w_words, w_scales, b, offs, o
             for u in range(PAIR):
                 pair = pair_of_planes(a, u, both_vector, f"pair_{a}_{u}")
                 nc.scalar.copy(grouped[a][:, :, PAIR * u : PAIR * (u + 1)], pair[:].rearrange("p e n -> p n e"))
-        first_words = keep.tile([P, S], U32, name="first_words", tag="x_1_0", align_bytes=64)
+        first_words = keep.tile([P, S], U32, name="first_words", tag="x_1_0", align_bytes=LOAD_ALIGN)
         quantize(0, 0, S, grouped[0][:], first_words[:])
 
         pair = pair_of_planes(LAST, 0, (nc.vector.tensor_copy, scalar_gather), "last_pair")
         for s in range(PARTS):
-            copy = nc.vector.tensor_copy if s < 2 else nc.scalar.copy
+            copy = nc.scalar.copy if s < 2 else nc.vector.tensor_copy
             copy(ends[s][:, :, 0:PAIR], pair[:, :, s * PART : (s + 1) * PART].rearrange("p e n -> p n e"))
-        held_words = keep.tile([P, S], U32, name="held_words", tag="x_2_0", align_bytes=64)
+        held_words = keep.tile([P, S], U32, name="held_words", tag="x_2_0", align_bytes=LOAD_ALIGN)
         quantize(1, 0, S, grouped[1][:], held_words[:])
-        late = [
-            shared.tile([P, PAIR * PART], BF16, name=f"late_{s}", align_bytes=64, offset=s * PAIR * PART * 2) for s in range(PARTS)
-        ]
-        for s in range(PARTS):
-            gather = nc.vector.tensor_copy if s < 2 else scalar_gather
-            gather(late[s][:, PART : PAIR * PART], picked_of(LAST, 3, s * PART, (s + 1) * PART))
+        late = shared.tile([P, PARTS - 2, PAIR, PART], BF16, name="late", align_bytes=64, offset=0)
+        for s in range(2):
+            scalar_gather(ends[s][:, :, 3], picked_of(LAST, 3, s * PART, (s + 1) * PART))
+        for s in range(2, PARTS):
+            nc.vector.tensor_copy(late[:, s - 2, 1, :], picked_of(LAST, 3, s * PART, (s + 1) * PART))
         for i in range(WARM_UPS):
             nc.tensor.matmul_mx(
                 out=banks[0][0][0:WARM_ROWS, :],
@@ -153,25 +153,22 @@ def tile_picked_pool_lin_gelu_sub_e_kernel(tc, xT, w_words, w_scales, b, offs, o
         for s in range(PARTS):
             multiply(1, s)
 
-        nc.vector.tensor_copy(late[0][:, 0 : PART // 2], picked_of(LAST, 2, 0, PART // 2))
-        scalar_gather(late[0][:, PART // 2 : PART], picked_of(LAST, 2, PART // 2, PART))
-        for s in range(1, PARTS):
-            gather = nc.vector.tensor_copy if s < 2 else scalar_gather
-            gather(late[s][:, 0:PART], picked_of(LAST, 2, s * PART, (s + 1) * PART))
+        for s in range(2):
+            scalar_gather(ends[s][:, :, 2], picked_of(LAST, 2, s * PART, (s + 1) * PART))
+        for s in range(2, PARTS):
+            nc.vector.tensor_copy(late[:, s - 2, 0, :], picked_of(LAST, 2, s * PART, (s + 1) * PART))
 
         last_words = [keep.tile([P, PART], U32, name=f"last_words_{s}", align_bytes=64) for s in range(PARTS)]
-
-        def weave(s, copy):
-            copy(ends[s][:, :, PAIR:PACK], late[s][:].rearrange("p (e n) -> p n e", e=PAIR))
 
         def close(s):
             quantize(LAST, s * PART, (s + 1) * PART, ends[s][:], last_words[s][:])
             multiply(0, s)
             multiply(LAST, s)
 
-        for s in range(PARTS):
-            weave(s, nc.vector.tensor_copy if s < 2 else nc.scalar.copy)
-        for s in range(PARTS):
+        close(0)
+        for s in range(2, PARTS):
+            nc.vector.tensor_copy(ends[s][:, :, PAIR:PACK], late[:, s - 2, :, :].rearrange("p e n -> p n e"))
+        for s in range(1, PARTS):
             close(s)
 
         def finish(m, s, first, last):

@@ -26,7 +26,7 @@ PARTS = S // PART
 PAIR = 2
 LOADS = (((0, 4),), ((0, 2), (2, 4)), ((0, 2), (3, 4), (2, 3)))
 PASS_ORDER = (1, 0, 2)
-WARM_UPS = 2
+WARM_WIDTHS = (512, 512, 128)
 WARM_ROWS = 32
 LOAD_ALIGN = 256
 BLOCK = 8
@@ -42,6 +42,7 @@ def tile_picked_pool_lin_gelu_sub_e_kernel(tc, xT, w_words, w_scales, b, offs, o
         offsets = keep.tile([P, S // 16], U16, name="offsets")
         w_codes = [keep.tile([P, N], I32, name=f"w_codes_{a}", align_bytes=LOAD_ALIGN) for a in range(PASSES)]
         w_scale = keep.tile([P, PASSES, N], U8, name="w_scale", align_bytes=64)
+        scale_rows = keep.tile([4, PASSES, 4, N // 4], I32, name="scale_rows", align_bytes=LOAD_ALIGN)
         bias = keep.tile([P, M_TILES, BLOCK], F32, name="bias")
         warm = keep.tile([P, 1], F32, name="warm")
         blocks = [
@@ -70,11 +71,12 @@ def tile_picked_pool_lin_gelu_sub_e_kernel(tc, xT, w_words, w_scales, b, offs, o
             nc.sync.dma_start(out=blocks[a][i][:], in_=x_view[a, :, first * T : last * T])
 
         load_block(0, 0)
+        nc.scalar.dma_start(
+            out=scale_rows[:].rearrange("r a q m -> r (a q) m"),
+            in_=w_scales.rearrange("a (q r) m -> r (a q) m", r=4).bitcast(I32),
+        )
         for q in range(4):
-            nc.scalar.dma_start(
-                out=w_scale[32 * q : 32 * q + 4, :, :].bitcast(I32),
-                in_=w_scales[:, 4 * q : 4 * q + 4, :].rearrange("a r m -> r a m").bitcast(I32),
-            )
+            nc.vector.tensor_copy(w_scale[32 * q : 32 * q + 4, :, :].bitcast(I32), scale_rows[:, :, q, :])
         nc.scalar.activation(warm[:], warm[:], GELU)
         nc.sync.dma_start(offsets[:], offs)
         for a, i in ((1, 0), (1, 1), (2, 0), (2, 1), (2, 2)):
@@ -130,23 +132,28 @@ def tile_picked_pool_lin_gelu_sub_e_kernel(tc, xT, w_words, w_scales, b, offs, o
         quantize(0, 0, S, grouped[0][:], first_words[:])
 
         pair = pair_of_planes(LAST, 0, (nc.vector.tensor_copy, scalar_gather), "last_pair")
-        for s in range(PARTS):
+
+        def lay_pair(s):
             copy = nc.scalar.copy if s < 2 else nc.vector.tensor_copy
             copy(ends[s][:, :, 0:PAIR], pair[:, :, s * PART : (s + 1) * PART].rearrange("p e n -> p n e"))
+
+        for s in range(PARTS - 1):
+            lay_pair(s)
         held_words = keep.tile([P, S], U32, name="held_words", tag="x_2_0", align_bytes=LOAD_ALIGN)
         quantize(1, 0, S, grouped[1][:], held_words[:])
+        lay_pair(PARTS - 1)
         late = shared.tile([P, PARTS - 2, PAIR, PART], BF16, name="late", align_bytes=64, offset=0)
         for s in range(2):
             scalar_gather(ends[s][:, :, 3], picked_of(LAST, 3, s * PART, (s + 1) * PART))
         for s in range(2, PARTS):
             nc.vector.tensor_copy(late[:, s - 2, 1, :], picked_of(LAST, 3, s * PART, (s + 1) * PART))
-        for i in range(WARM_UPS):
+        for width in WARM_WIDTHS:
             nc.tensor.matmul_mx(
-                out=banks[0][0][0:WARM_ROWS, :],
+                out=banks[0][0][0:WARM_ROWS, 0:width],
                 lhsT=held_words[:, 0:WARM_ROWS].bitcast(FP8X4),
                 lhsT_scale=scales[1][:, 0:WARM_ROWS],
-                rhs=held_words[:].bitcast(FP8X4),
-                rhs_scale=scales[1][:],
+                rhs=held_words[:, 0:width].bitcast(FP8X4),
+                rhs_scale=scales[1][:, 0:width],
                 start=True,
                 stop=True,
             )

from contextlib import ExitStack

import concourse.mybir as mybir

K, T, S, N, D = 1536, 2048, 512, 256, 8
FLOPS = 2 * K * S * N

F32 = mybir.dt.float32
BF16 = mybir.dt.bfloat16
U32 = mybir.dt.uint32
I32 = mybir.dt.int32
U16 = mybir.dt.uint16
U8 = mybir.dt.uint8
FP8X4 = mybir.dt.float8_e4m3fn_x4
GELU = mybir.ActivationFunctionType.Gelu_apprx_tanh
COPY = mybir.ActivationFunctionType.Copy

P = 128
PACK = 4
PASSES = K // (P * PACK)
LAST = PASSES - 1
M_TILES = N // P
HALF = S // 2
PART = 128
PARTS = S // PART
PAIR = 2
LOADS = (((0, 4),), ((0, 2), (2, 4)), ((0, 2), (3, 4), (2, 3)))
PASS_ORDER = (1, 0, 2)
WARM_WIDTHS = (512, 512, 128)
WARM_ROWS = 32
LOAD_ALIGN = 256
BLOCK = 8


def tile_picked_pool_lin_gelu_sub_e_kernel(tc, xT, w_words, w_scales, b, offs, out):
    nc = tc.nc
    with ExitStack() as ctx:
        keep = ctx.enter_context(tc.tile_pool(name="keep", bufs=1))
        shared = ctx.enter_context(tc.tile_pool(name="shared", bufs=1))
        psum = ctx.enter_context(tc.psum_pool(name="psum", bufs=1))

        offsets = keep.tile([P, S // 16], U16, name="offsets")
        w_codes = [keep.tile([P, N], I32, name=f"w_codes_{a}", align_bytes=LOAD_ALIGN) for a in range(PASSES)]
        w_scale = keep.tile([P, PASSES, N], U8, name="w_scale", align_bytes=64)
        scale_rows = keep.tile([4, PASSES, 4, N // 4], I32, name="scale_rows", align_bytes=LOAD_ALIGN)
        bias = keep.tile([P, M_TILES, BLOCK], F32, name="bias")
        warm = keep.tile([P, 1], F32, name="warm")
        blocks = [
            [keep.tile([P, (last - first) * T], F32, name=f"x_{a}_{first}", tag=f"x_{a}_{first}", align_bytes=LOAD_ALIGN) for first, last in LOADS[a]]
            for a in range(PASSES)
        ]
        grouped = [
            keep.tile([P, S, PACK], BF16, name="grouped_0", align_bytes=64),
            shared.tile([P, S, PACK], BF16, name="grouped_1", align_bytes=64, offset=0),
        ]
        ends = [keep.tile([P, PART, PACK], BF16, name=f"ends_{s}", align_bytes=64) for s in range(PARTS)]
        scales = [keep.tile([P, S], U8, name=f"scales_{a}", align_bytes=64) for a in range(PASSES)]
        banks = [[psum.tile([P, S], F32, name=f"acc_{m}_{s}") for s in range(PARTS)] for m in range(M_TILES)]
        act = [[keep.tile([P, PART], F32, name=f"act_{m}_{s}") for s in range(PARTS)] for m in range(M_TILES)]
        pooled = keep.tile([P, M_TILES, S // D], F32, name="pooled", align_bytes=64)
        codes = {}

        nc.gpsimd.memset(w_scale[:].bitcast(I32), 0)
        nc.gpsimd.memset(warm[:], 0.0)

        x_view = xT.rearrange("(a p j) t -> a p (j t)", p=P, j=PACK)
        w_view = w_words.rearrange("a p m r -> a p (m r)").bitcast(I32)

        def load_block(a, i):
            first, last = LOADS[a][i]
            nc.sync.dma_start(out=blocks[a][i][:], in_=x_view[a, :, first * T : last * T])

        load_block(0, 0)
        nc.scalar.dma_start(
            out=scale_rows[:].rearrange("r a q m -> r (a q) m"),
            in_=w_scales.rearrange("a (q r) m -> r (a q) m", r=4).bitcast(I32),
        )
        for q in range(4):
            nc.vector.tensor_copy(w_scale[32 * q : 32 * q + 4, :, :].bitcast(I32), scale_rows[:, :, q, :])
        nc.scalar.activation(warm[:], warm[:], GELU)
        nc.sync.dma_start(offsets[:], offs)
        for a, i in ((1, 0), (1, 1), (2, 0), (2, 1), (2, 2)):
            load_block(a, i)
        for a in (1, 2, 0):
            nc.sync.dma_start(out=w_codes[a][:], in_=w_view[a])
        with nc.allow_non_contiguous_dma(reason="one bias value a partition"):
            nc.sync.dma_start(out=bias[:, :, 0:1], in_=b.rearrange("(m p) o -> p m o", p=P))

        def picked_of(a, j, first, last):
            for (low, high), block in zip(LOADS[a], blocks[a]):
                if low <= j < high:
                    return block[:, (j - low) * T : (j - low + 1) * T].indirect(offsets[:, first // 16 : last // 16])

        def scalar_gather(dst, src):
            nc.scalar.activation(dst, src, COPY)

        def quantize(a, first, last, values, words):
            for s in range(first // PART, last // PART):
                codes[a, s] = words[:, s * PART - first : (s + 1) * PART - first]
            nc.vector.quantize_mx(
                out=words.bitcast(FP8X4),
                scales=scales[a][:, first:last],
                in_=values.rearrange("p n j -> p (n j)"),
            )

        def multiply(a, s):
            cols = slice(s * PART, (s + 1) * PART)
            for m in range(M_TILES):
                rows = slice(m * P, (m + 1) * P)
                nc.tensor.matmul_mx(
                    out=banks[m][s][:, 0:PART],
                    lhsT=w_codes[a][:, rows].bitcast(FP8X4),
                    lhsT_scale=w_scale[:, a, rows],
                    rhs=codes[a, s].bitcast(FP8X4),
                    rhs_scale=scales[a][:, cols],
                    start=(a == PASS_ORDER[0]),
                    stop=(a == LAST),
                )

        def pair_of_planes(a, u, engines, tag):
            pair = keep.tile([P, PAIR, S], F32, name=f"pair_{a}_{u}", tag=tag, align_bytes=64)
            for e, gather in enumerate(engines):
                gather(pair[:, e, :], picked_of(a, PAIR * u + e, 0, S))
            return pair

        both_vector = (nc.vector.tensor_copy, nc.vector.tensor_copy)
        for a in range(LAST):
            for u in range(PAIR):
                pair = pair_of_planes(a, u, both_vector, f"pair_{a}_{u}")
                nc.scalar.copy(grouped[a][:, :, PAIR * u : PAIR * (u + 1)], pair[:].rearrange("p e n -> p n e"))
        first_words = keep.tile([P, S], U32, name="first_words", tag="x_1_0", align_bytes=LOAD_ALIGN)
        quantize(0, 0, S, grouped[0][:], first_words[:])

        pair = pair_of_planes(LAST, 0, (nc.vector.tensor_copy, scalar_gather), "last_pair")

        def lay_pair(s):
            copy = nc.scalar.copy if s < 2 else nc.vector.tensor_copy
            copy(ends[s][:, :, 0:PAIR], pair[:, :, s * PART : (s + 1) * PART].rearrange("p e n -> p n e"))

        for s in range(PARTS - 1):
            lay_pair(s)
        held_words = keep.tile([P, S], U32, name="held_words", tag="x_2_0", align_bytes=LOAD_ALIGN)
        quantize(1, 0, S, grouped[1][:], held_words[:])
        lay_pair(PARTS - 1)
        late = shared.tile([P, PARTS - 2, PAIR, PART], BF16, name="late", align_bytes=64, offset=0)
        for s in range(2):
            scalar_gather(ends[s][:, :, 3], picked_of(LAST, 3, s * PART, (s + 1) * PART))
        for s in range(2, PARTS):
            nc.vector.tensor_copy(late[:, s - 2, 1, :], picked_of(LAST, 3, s * PART, (s + 1) * PART))
        for width in WARM_WIDTHS:
            nc.tensor.matmul_mx(
                out=banks[0][0][0:WARM_ROWS, 0:width],
                lhsT=held_words[:, 0:WARM_ROWS].bitcast(FP8X4),
                lhsT_scale=scales[1][:, 0:WARM_ROWS],
                rhs=held_words[:, 0:width].bitcast(FP8X4),
                rhs_scale=scales[1][:, 0:width],
                start=True,
                stop=True,
            )
        for s in range(PARTS):
            multiply(1, s)

        for s in range(2):
            scalar_gather(ends[s][:, :, 2], picked_of(LAST, 2, s * PART, (s + 1) * PART))
        for s in range(2, PARTS):
            nc.vector.tensor_copy(late[:, s - 2, 0, :], picked_of(LAST, 2, s * PART, (s + 1) * PART))

        last_words = [keep.tile([P, PART], U32, name=f"last_words_{s}", align_bytes=64) for s in range(PARTS)]

        def close(s):
            quantize(LAST, s * PART, (s + 1) * PART, ends[s][:], last_words[s][:])
            multiply(0, s)
            multiply(LAST, s)

        close(0)
        for s in range(2, PARTS):
            nc.vector.tensor_copy(ends[s][:, :, PAIR:PACK], late[:, s - 2, :, :].rearrange("p e n -> p n e"))
        for s in range(1, PARTS):
            close(s)

        def finish(m, s, first, last):
            nc.scalar.activation(act[m][s][:, first:last], banks[m][s][:, first:last], GELU, bias=bias[:, m, 0:1])
            nc.vector.tensor_reduce(
                out=pooled[:, m, (s * PART + first) // D : (s * PART + last) // D],
                in_=act[m][s][:, first:last].rearrange("p (v d) -> p v d", d=D),
                op=mybir.AluOpType.max,
                axis=mybir.AxisListType.X,
            )

        for s in range(PARTS):
            for m in range(M_TILES):
                if (s, m) == (PARTS - 1, M_TILES - 1):
                    finish(m, s, 0, PART // 2)
                    finish(m, s, PART // 2, PART)
                else:
                    finish(m, s, 0, PART)
        nc.sync.dma_start(out=out.rearrange("(m p) v -> p m v", p=P), in_=pooled[:])
